import numpy as np
import ml_dtypes


def mxq(x, axis, fmt="e4m3"):
    dtype, down = {"e4m3": (ml_dtypes.float8_e4m3fn, 7), "e5m2": (ml_dtypes.float8_e5m2, 14)}[fmt]
    v = np.moveaxis(np.asarray(x, np.float32).astype(ml_dtypes.bfloat16).astype(np.float64), axis, -1)
    blocks = v.reshape(v.shape[:-1] + (-1, 32))
    amax = np.abs(blocks).max(-1, keepdims=True)
    byte = np.maximum(np.where(amax > 0, np.frexp(amax)[1] - 1 + 127, 0) - down, 1)
    scale = np.exp2(byte - 127.0)
    codes = (blocks / scale).astype(np.float32).astype(dtype).astype(np.float64)
    return np.moveaxis((codes * scale).reshape(v.shape), -1, axis)


WIDE = False


def mx_kscale(k):
    if not WIDE:
        return np.ones(k)
    levels = np.array([10, -10, 5, -5, 0])
    if k % 512:
        return np.exp2(np.random.permutation(np.resize(levels, k // 32))).repeat(32)
    a = np.empty((k // 512, 16))
    for p in range(k // 512):
        a[p, :8] = np.random.permutation(np.resize(levels, 8))
        for g in range(8):
            far = levels[np.abs(levels - a[p, g]) >= 10]
            a[p, g + 8] = far[np.random.randint(len(far))]
    return np.exp2(a.ravel()).repeat(32)


def f64(x):
    return np.asarray(x).astype(np.float64)


def striped(idx):
    return np.tile(idx.reshape(-1, 16).T, (8, 1)).astype(np.uint16)


def unstriped(offs):
    return offs[:16].T.reshape(-1).astype(np.int64)


E2M1 = np.array([0.0, 0.5, 1.0, 1.5, 2.0, 3.0, 4.0, 6.0, -0.0, -0.5, -1.0, -1.5, -2.0, -3.0, -4.0, -6.0])


def pack_weight(w, fmt):
    k, n = w.shape
    w = f64(np.asarray(w, np.float32).astype(ml_dtypes.bfloat16)).reshape(k // 32, 32, n)
    amax = np.abs(w).max(1)
    if fmt == "e4m3":
        byte = np.frexp(amax)[1] - 1 + 127 - 7
    else:
        mant, ex = np.frexp(amax / 6.0)
        byte = np.where(mant > 0.5, ex, ex - 1) + 127
    byte = np.clip(np.where(amax > 0, byte, 1), 1, 254)
    scaled = (w * np.exp2(127.0 - byte)[:, None, :]).reshape(k, n).astype(np.float32)
    by_word = np.ascontiguousarray(scaled.reshape(k // 512, 128, 4, n).transpose(0, 1, 3, 2))
    if fmt == "e4m3":
        words = by_word.astype(ml_dtypes.float8_e4m3fn).view(np.uint8)
    else:
        c = by_word.astype(ml_dtypes.float4_e2m1fn).view(np.uint8) & 0xF
        words = (c[..., 0::2] | (c[..., 1::2] << 4)).reshape(k // 512, 128, 2 * n)
    return np.ascontiguousarray(words), np.ascontiguousarray(byte.astype(np.uint8).reshape(k // 512, 16, n))


def unpack_weight(words, scales, fmt):
    g, _, n = scales.shape
    words = np.ascontiguousarray(words).reshape(g, 128, n, -1)
    if fmt == "e4m3":
        vals = words.view(ml_dtypes.float8_e4m3fn).astype(np.float64)
    else:
        nib = np.empty((g, 128, n, 4), np.uint8)
        nib[..., 0::2] = words & 0xF
        nib[..., 1::2] = words >> 4
        vals = E2M1[nib]
    vals = vals * np.repeat(np.exp2(scales.astype(np.float64) - 127.0), 8, axis=1)[..., None]
    return vals.transpose(0, 1, 3, 2).reshape(g * 512, n)


def gelu(v):
    return 0.5 * v * (1.0 + np.tanh(np.sqrt(2.0 / np.pi) * (v + 0.044715 * v**3)))


K, H, T, S = 512, 1024, 2048, 1024


def setup_inputs():
    n = np.random.standard_normal
    s = mx_kscale(K)[:, None]
    u = mx_kscale(H)[:, None]
    ground = np.abs(n((K, T)))
    snapshot = np.abs(ground + 0.5 * n((K, T)))
    tab_words, tab_scales = pack_weight(snapshot * s, "e4m3")
    resp = n((K, H)) / np.sqrt(K)
    back_words, back_scales = pack_weight(resp.T / u, "e4m3")
    return {
        "tab_words": tab_words, "tab_scales": tab_scales,
        "offs": striped(np.random.permutation(T)[:S]),
        "gT": ground.astype(np.float32),
        "gm": (resp * u.T / s).astype(np.float32),
        "field": (n((H, S)) * u).astype(np.float32),
        "back_words": back_words, "back_scales": back_scales,
        "step": np.random.uniform(0.1, 0.3, K).astype(np.float32),
    }


def reference(tab_words, tab_scales, offs, gT, gm, field, back_words, back_scales, step):
    v = unpack_weight(tab_words, tab_scales, "e4m3")[:, unstriped(offs)]
    pred = mxq(f64(gm), 0, "e4m3").T @ v
    h = f64(field) - pred
    y = unpack_weight(back_words, back_scales, "e4m3").T @ mxq(h, 0, "e4m3")
    g = f64(gT)[:, unstriped(offs)]
    new = np.maximum(g + f64(step)[:, None] * y, 0.0)
    out = f64(gT).copy()
    out[:, unstriped(offs)] = new
    return out

@@ -1,0 +1,210 @@
+from contextlib import ExitStack
+
+import concourse.mybir as mybir
+
+K, H, T, S = 512, 1024, 2048, 1024
+FLOPS = 2 * K * H * S + 2 * H * K * S
+
+F32 = mybir.dt.float32
+BF16 = mybir.dt.bfloat16
+I32 = mybir.dt.int32
+U32 = mybir.dt.uint32
+U16 = mybir.dt.uint16
+U8 = mybir.dt.uint8
+FP8X4 = mybir.dt.float8_e4m3fn_x4
+ALU = mybir.AluOpType
+ACT = mybir.ActivationFunctionType
+
+P = 128
+PACK = 4
+PASS = P * PACK
+PASSES = H // PASS
+TILES = K // P
+CHUNKS = ((0, 256), (256, 512), (512, 1024))
+
+
+def tile_list_villa_survey_step_kernel(
+    tc, tab_words, tab_scales, offs, gT, gm, field, back_words, back_scales, step, out
+):
+    nc = tc.nc
+    with ExitStack() as ctx:
+        keep = ctx.enter_context(tc.tile_pool(name="keep", bufs=1))
+        pred_psum = ctx.enter_context(tc.psum_pool(name="pred_psum", bufs=4))
+        y_psum = ctx.enter_context(tc.psum_pool(name="y_psum", bufs=4))
+
+        def sb(name, shape, dtype):
+            return keep.tile(shape, dtype, name=name, tag=name, align_bytes=64)
+
+        offsets = keep.tile([P, S // 16], U16, name="offsets")
+        table_scales = sb("table_scales", [P, T], U8)
+        table_words = sb("table_words", [P, T], I32)
+        b_scales = sb("b_scales", [P, PASSES * K], U8)
+        b_words = sb("b_words", [P, PASSES * K], I32)
+        steps = sb("steps", [P, TILES], F32)
+        maps = [sb("map%d" % i, [P, T], F32) for i in range(TILES)]
+        gm_raw = [sb("gm_raw%d" % q, [P, PACK, 256], F32) for q in range(4)]
+        gm_bf = [sb("gm_bf%d" % a, [P, PASS * PACK], BF16) for a in range(PASSES)]
+        gm_codes = [sb("gm_codes%d" % a, [P, PASS], U32) for a in range(PASSES)]
+        gm_scales = [sb("gm_scales%d" % a, [P, PASS], U8) for a in range(PASSES)]
+        v_words = sb("v_words", [P, S], U32)
+        v_scales = sb("v_scales", [P, S], U8)
+        h_codes = [sb("h_codes%d" % a, [P, S], U32) for a in range(PASSES)]
+        h_scales = [sb("h_scales%d" % a, [P, S], U8) for a in range(PASSES)]
+        fields = {}
+        h_bf = {}
+        for c, (j0, j1) in enumerate(CHUNKS):
+            for a in range(PASSES):
+                fields[c, a] = sb("field%d_%d" % (c, a), [P, PACK, j1 - j0], F32)
+                h_bf[c, a] = sb("h_bf%d_%d" % (c, a), [P, (j1 - j0) * PACK], BF16)
+
+        nc.vector.memset(table_scales[:].bitcast(I32), 0)
+        nc.gpsimd.memset(b_scales[:].bitcast(I32), 0)
+
+        def load_gm(q):
+            nc.sync.dma_start(gm_raw[q][:], gm[:, 256 * q : 256 * (q + 1)].rearrange("(p j) c -> p j c", j=PACK))
+
+        def load_field(c, a):
+            j0, j1 = CHUNKS[c]
+            rows = field[PASS * a : PASS * (a + 1), j0:j1]
+            nc.sync.dma_start(fields[c, a][:], rows.rearrange("(p t) j -> p t j", t=PACK))
+
+        def load_map(i):
+            nc.sync.dma_start(maps[i][:], gT[P * i : P * (i + 1), :])
+
+        nc.sync.dma_start(offsets[:], offs)
+        for quad in range(4):
+            nc.sync.dma_start(
+                table_scales[32 * quad : 32 * quad + 4, :].bitcast(I32),
+                tab_scales[0, 4 * quad : 4 * quad + 4, :].bitcast(I32),
+            )
+        nc.sync.dma_start(table_words[:], tab_words[0].rearrange("p t i -> p (t i)").bitcast(I32))
+        for q in range(4):
+            load_gm(q)
+        load_field(0, 0)
+        load_field(0, 1)
+        for quad in range(4):
+            nc.sync.dma_start(
+                b_scales[32 * quad : 32 * quad + 4, :].bitcast(I32).rearrange("r (a c) -> r a c", a=PASSES),
+                back_scales[:, 4 * quad : 4 * quad + 4, :].bitcast(I32).rearrange("a r c -> r a c"),
+            )
+        with nc.allow_non_contiguous_dma(reason="one step to a partition and tile"):
+            nc.sync.dma_start(steps[:], step.rearrange("(i p) -> p i", p=P))
+        nc.sync.dma_start(
+            b_words[:].rearrange("p (a c) -> p a c", a=PASSES),
+            back_words.rearrange("a p c i -> p a (c i)").bitcast(I32),
+        )
+        load_map(0)
+        load_field(1, 0)
+        load_field(1, 1)
+        load_map(1)
+        load_map(2)
+        load_field(2, 0)
+        load_field(2, 1)
+        load_map(3)
+
+        nc.vector.tensor_copy(v_scales[:], table_scales[:].indirect(offsets[:]))
+        nc.vector.tensor_copy(v_words[:], table_words[:].bitcast(U32).indirect(offsets[:]))
+
+        def weave_gm(q):
+            a, half = divmod(q, 2)
+            dst = gm_bf[a][:].rearrange("p (t m j) -> p m j t", t=PACK, j=PACK)[:, 64 * half : 64 * (half + 1)]
+            src = gm_raw[q][:].rearrange("p j (m t) -> p m j t", t=PACK)
+            if q == 3:
+                nc.vector.tensor_copy(dst, src)
+            else:
+                nc.scalar.copy(dst, src)
+
+        def quantize_gm(a):
+            nc.vector.quantize_mx(out=gm_codes[a][:].bitcast(FP8X4), scales=gm_scales[a][:], in_=gm_bf[a][:])
+
+        def residual(c, a):
+            j0, j1 = CHUNKS[c]
+            for b in range((j1 - j0) // P):
+                cols = slice(j0 + P * b, j0 + P * (b + 1))
+                pred = pred_psum.tile([P, PACK, P], F32, name="pred")
+                for t in range(PACK):
+                    nc.tensor.matmul_mx(
+                        out=pred[:, t, :],
+                        lhsT=gm_codes[a][:, P * t : P * (t + 1)].bitcast(FP8X4),
+                        lhsT_scale=gm_scales[a][:, P * t : P * (t + 1)],
+                        rhs=v_words[:, cols].bitcast(FP8X4),
+                        rhs_scale=v_scales[:, cols],
+                        start=True,
+                        stop=True,
+                    )
+                dst = h_bf[c, a][:, PASS * b : PASS * (b + 1)].rearrange("p (g i t) -> p g t i", i=4, t=PACK)
+                measured = fields[c, a][:, :, P * b : P * (b + 1)].rearrange("p t (g i) -> p g t i", i=4)
+                nc.vector.tensor_tensor(dst, measured, pred[:].rearrange("p t (g i) -> p g t i", i=4), ALU.subtract)
+
+        def quantize_h(c, a):
+            j0, j1 = CHUNKS[c]
+            nc.vector.quantize_mx(
+                out=h_codes[a][:, j0:j1].bitcast(FP8X4), scales=h_scales[a][:, j0:j1], in_=h_bf[c, a][:]
+            )
+
+        moved = {}
+
+        def gather_move(i, j0, j1):
+            width = j1 - j0
+            y = y_psum.tile([P, width], F32, name="y")
+            for a in range(PASSES):
+                cols = slice(K * a + P * i, K * a + P * (i + 1))
+                nc.tensor.matmul_mx(
+                    out=y[:],
+                    lhsT=b_words[:, cols].bitcast(FP8X4),
+                    lhsT_scale=b_scales[:, cols],
+                    rhs=h_codes[a][:, j0:j1].bitcast(FP8X4),
+                    rhs_scale=h_scales[a][:, j0:j1],
+                    start=(a == 0),
+                    stop=(a == PASSES - 1),
+                )
+            scaled = sb("scaled%d_%d" % (i, j0), [P, width], F32)
+            nc.scalar.activation(scaled[:], y[:], ACT.Copy, scale=steps[:, i : i + 1])
+            summed = sb("summed%d_%d" % (i, j0), [P, width], F32)
+            nc.vector.tensor_tensor(
+                summed[:], maps[i][:].indirect(offsets[:, j0 // 16 : j1 // 16]), scaled[:], ALU.add
+            )
+            new = sb("new%d_%d" % (i, j0), [P, width], F32)
+            nc.scalar.activation(new[:], summed[:], ACT.Relu)
+            moved[i, j0] = new
+
+        def scatter(i, j0, j1):
+            nc.vector.tensor_copy(maps[i][:].indirect(offsets[:, j0 // 16 : j1 // 16]), moved[i, j0][:])
+            if j1 == S:
+                nc.sync.dma_start(out[P * i : P * (i + 1), :], maps[i][:])
+
+        weave_gm(0)
+        weave_gm(1)
+        quantize_gm(0)
+        weave_gm(2)
+        weave_gm(3)
+        quantize_gm(1)
+        residual(0, 0)
+        residual(0, 1)
+        quantize_h(0, 0)
+        quantize_h(0, 1)
+        gather_move(0, 0, 256)
+        residual(1, 0)
+        scatter(0, 0, 256)
+        residual(1, 1)
+        gather_move(1, 0, 256)
+        quantize_h(1, 0)
+        quantize_h(1, 1)
+        scatter(1, 0, 256)
+        gather_move(0, 256, 512)
+        gather_move(1, 256, 512)
+        scatter(0, 256, 512)
+        gather_move(2, 0, 512)
+        scatter(1, 256, 512)
+        residual(2, 0)
+        scatter(2, 0, 512)
+        gather_move(3, 0, 512)
+        residual(2, 1)
+        quantize_h(2, 0)
+        quantize_h(2, 1)
+        scatter(3, 0, 512)
+        gather_move(0, 512, 1024)
+        for i in range(TILES):
+            if i + 1 < TILES:
+                gather_move(i + 1, 512, 1024)
+            scatter(i, 512, 1024)

@@ -1,6 +1,7 @@
 from contextlib import ExitStack
 
 import concourse.mybir as mybir
+from concourse.masks import make_identity
 
 K, H, T, S = 512, 1024, 2048, 1024
 FLOPS = 2 * K * H * S + 2 * H * K * S
@@ -20,7 +21,8 @@ PACK = 4
 PASS = P * PACK
 PASSES = H // PASS
 TILES = K // P
-CHUNKS = ((0, 256), (256, 512), (512, 1024))
+SCALAR_SHARE = 44
+CHUNKS = ((0, 256), (256, 512), (512, 768), (768, 1024))
 
 
 def tile_list_villa_survey_step_kernel(
@@ -29,11 +31,12 @@ def tile_list_villa_survey_step_kernel(
     nc = tc.nc
     with ExitStack() as ctx:
         keep = ctx.enter_context(tc.tile_pool(name="keep", bufs=1))
-        pred_psum = ctx.enter_context(tc.psum_pool(name="pred_psum", bufs=4))
-        y_psum = ctx.enter_context(tc.psum_pool(name="y_psum", bufs=4))
+        pred_psum = ctx.enter_context(tc.psum_pool(name="pred_psum", bufs=3))
+        turn_psum = ctx.enter_context(tc.psum_pool(name="turn_psum", bufs=3))
+        y_psum = ctx.enter_context(tc.psum_pool(name="y_psum", bufs=2))
 
-        def sb(name, shape, dtype):
-            return keep.tile(shape, dtype, name=name, tag=name, align_bytes=64)
+        def sb(name, shape, dtype, tag=None):
+            return keep.tile(shape, dtype, name=name, tag=tag or name, align_bytes=64)
 
         offsets = keep.tile([P, S // 16], U16, name="offsets")
         table_scales = sb("table_scales", [P, T], U8)
@@ -42,77 +45,98 @@ def tile_list_villa_survey_step_kernel(
         b_words = sb("b_words", [P, PASSES * K], I32)
         steps = sb("steps", [P, TILES], F32)
         maps = [sb("map%d" % i, [P, T], F32) for i in range(TILES)]
-        gm_raw = [sb("gm_raw%d" % q, [P, PACK, 256], F32) for q in range(4)]
+        gm_raw = [sb("gm_raw%d" % a, [P, PACK, PASS], F32) for a in range(PASSES)]
         gm_bf = [sb("gm_bf%d" % a, [P, PASS * PACK], BF16) for a in range(PASSES)]
         gm_codes = [sb("gm_codes%d" % a, [P, PASS], U32) for a in range(PASSES)]
         gm_scales = [sb("gm_scales%d" % a, [P, PASS], U8) for a in range(PASSES)]
         v_words = sb("v_words", [P, S], U32)
         v_scales = sb("v_scales", [P, S], U8)
-        h_codes = [sb("h_codes%d" % a, [P, S], U32) for a in range(PASSES)]
-        h_scales = [sb("h_scales%d" % a, [P, S], U8) for a in range(PASSES)]
+        identity = sb("identity", [P, P], F32)
         fields = {}
-        h_bf = {}
+        h_bf, h_codes, h_scales = [], [], []
         for c, (j0, j1) in enumerate(CHUNKS):
+            h_bf.append(sb("h_bf%d" % c, [P, PASSES * (j1 - j0) * PACK], BF16))
+            h_codes.append(sb("h_codes%d" % c, [P, PASSES * (j1 - j0)], U32))
+            h_scales.append(sb("h_scales%d" % c, [P, PASSES * (j1 - j0)], U8))
+        field_tiles = {}
+        for half in range(2):
             for a in range(PASSES):
-                fields[c, a] = sb("field%d_%d" % (c, a), [P, PACK, j1 - j0], F32)
-                h_bf[c, a] = sb("h_bf%d_%d" % (c, a), [P, (j1 - j0) * PACK], BF16)
+                field_tiles[half, a] = sb("field%d_%d" % (half, a), [P, PACK, 512], F32)
+                for c in (2 * half, 2 * half + 1):
+                    fields[c, a] = field_tiles[half, a][:, :, 256 * (c % 2) : 256 * (c % 2 + 1)]
 
-        nc.vector.memset(table_scales[:].bitcast(I32), 0)
-        nc.gpsimd.memset(b_scales[:].bitcast(I32), 0)
+        nc.gpsimd.memset(table_scales[:].bitcast(I32), 0)
+        nc.vector.memset(b_scales[:].bitcast(I32), 0)
+        make_identity(nc, identity[:])
+        step_rows = sb("step_rows", [P, P], F32)
+        nc.gpsimd.memset(step_rows[:], 0.0)
 
-        def load_gm(q):
-            nc.sync.dma_start(gm_raw[q][:], gm[:, 256 * q : 256 * (q + 1)].rearrange("(p j) c -> p j c", j=PACK))
+        def load_gm(a, lo=0, hi=PASS):
+            columns = gm[:, PASS * a + lo : PASS * a + hi]
+            nc.sync.dma_start(gm_raw[a][:, :, lo:hi], columns.rearrange("(p j) c -> p j c", j=PACK))
 
-        def load_field(c, a):
-            j0, j1 = CHUNKS[c]
-            rows = field[PASS * a : PASS * (a + 1), j0:j1]
-            nc.sync.dma_start(fields[c, a][:], rows.rearrange("(p t) j -> p t j", t=PACK))
+        def load_field(half, a, lo=0, hi=512):
+            rows = field[PASS * a : PASS * (a + 1), 512 * half + lo : 512 * half + hi]
+            nc.sync.dma_start(field_tiles[half, a][:, :, lo:hi], rows.rearrange("(p t) j -> p t j", t=PACK))
+
+        def load_step():
+            nc.sync.dma_start(step_rows[:TILES, :], step.rearrange("(i p) -> i p", p=P))
+            step_turned = turn_psum.tile([P, P], F32, name="turn")
+            nc.tensor.transpose(step_turned[:], step_rows[:], identity[:])
+            nc.scalar.copy(steps[:], step_turned[:, :TILES])
+
+        def load_table_scales():
+            for quad in range(4):
+                nc.sync.dma_start(
+                    table_scales[32 * quad : 32 * quad + 4, :].bitcast(I32),
+                    tab_scales[0, 4 * quad : 4 * quad + 4, :].bitcast(I32),
+                )
+
+        def load_table_words():
+            nc.sync.dma_start(table_words[:], tab_words[0].rearrange("p t i -> p (t i)").bitcast(I32))
+
+        def load_back_scales():
+            for quad in range(4):
+                nc.sync.dma_start(
+                    b_scales[32 * quad : 32 * quad + 4, :].bitcast(I32).rearrange("r (a c) -> r a c", a=PASSES),
+                    back_scales[:, 4 * quad : 4 * quad + 4, :].bitcast(I32).rearrange("a r c -> r a c"),
+                )
+
+        def load_back_words(lo=0, hi=K):
+            nc.sync.dma_start(
+                b_words[:].rearrange("p (a c) -> p a c", a=PASSES)[:, :, lo:hi],
+                back_words.rearrange("a p c i -> p a (c i)").bitcast(I32)[:, :, lo:hi],
+            )
 
         def load_map(i):
             nc.sync.dma_start(maps[i][:], gT[P * i : P * (i + 1), :])
 
         nc.sync.dma_start(offsets[:], offs)
-        for quad in range(4):
-            nc.sync.dma_start(
-                table_scales[32 * quad : 32 * quad + 4, :].bitcast(I32),
-                tab_scales[0, 4 * quad : 4 * quad + 4, :].bitcast(I32),
-            )
-        nc.sync.dma_start(table_words[:], tab_words[0].rearrange("p t i -> p (t i)").bitcast(I32))
-        for q in range(4):
-            load_gm(q)
+        load_table_words()
+        load_table_scales()
+        load_gm(0)
+        load_gm(1)
+        load_step()
         load_field(0, 0)
         load_field(0, 1)
-        for quad in range(4):
-            nc.sync.dma_start(
-                b_scales[32 * quad : 32 * quad + 4, :].bitcast(I32).rearrange("r (a c) -> r a c", a=PASSES),
-                back_scales[:, 4 * quad : 4 * quad + 4, :].bitcast(I32).rearrange("a r c -> r a c"),
-            )
-        with nc.allow_non_contiguous_dma(reason="one step to a partition and tile"):
-            nc.sync.dma_start(steps[:], step.rearrange("(i p) -> p i", p=P))
-        nc.sync.dma_start(
-            b_words[:].rearrange("p (a c) -> p a c", a=PASSES),
-            back_words.rearrange("a p c i -> p a (c i)").bitcast(I32),
-        )
+        load_back_scales()
+        load_back_words(0, 256)
         load_map(0)
-        load_field(1, 0)
-        load_field(1, 1)
         load_map(1)
+        load_back_words(256, 512)
+        load_field(1, 0)
         load_map(2)
-        load_field(2, 0)
-        load_field(2, 1)
+        load_field(1, 1)
         load_map(3)
 
         nc.vector.tensor_copy(v_scales[:], table_scales[:].indirect(offsets[:]))
         nc.vector.tensor_copy(v_words[:], table_words[:].bitcast(U32).indirect(offsets[:]))
 
-        def weave_gm(q):
-            a, half = divmod(q, 2)
-            dst = gm_bf[a][:].rearrange("p (t m j) -> p m j t", t=PACK, j=PACK)[:, 64 * half : 64 * (half + 1)]
-            src = gm_raw[q][:].rearrange("p j (m t) -> p m j t", t=PACK)
-            if q == 3:
-                nc.vector.tensor_copy(dst, src)
-            else:
-                nc.scalar.copy(dst, src)
+        def weave_gm(a):
+            dst = gm_bf[a][:].rearrange("p (t m j) -> p m j t", t=PACK, j=PACK)
+            src = gm_raw[a][:].rearrange("p j (m t) -> p m j t", t=PACK)
+            nc.scalar.copy(dst[:, :SCALAR_SHARE], src[:, :SCALAR_SHARE])
+            nc.vector.tensor_copy(dst[:, SCALAR_SHARE:], src[:, SCALAR_SHARE:])
 
         def quantize_gm(a):
             nc.vector.quantize_mx(out=gm_codes[a][:].bitcast(FP8X4), scales=gm_scales[a][:], in_=gm_bf[a][:])
@@ -132,79 +156,171 @@ def tile_list_villa_survey_step_kernel(
                         start=True,
                         stop=True,
                     )
-                dst = h_bf[c, a][:, PASS * b : PASS * (b + 1)].rearrange("p (g i t) -> p g t i", i=4, t=PACK)
-                measured = fields[c, a][:, :, P * b : P * (b + 1)].rearrange("p t (g i) -> p g t i", i=4)
-                nc.vector.tensor_tensor(dst, measured, pred[:].rearrange("p t (g i) -> p g t i", i=4), ALU.subtract)
+                at = PACK * ((j1 - j0) * a + P * b)
+                dst = h_bf[c][:, at : at + PASS].rearrange("p (g i t) -> p g t i", i=2, t=PACK)
+                measured = fields[c, a][:, :, P * b : P * (b + 1)].rearrange("p t (g i) -> p g t i", i=2)
+                nc.vector.tensor_tensor(dst, measured, pred[:].rearrange("p t (g i) -> p g t i", i=2), ALU.subtract)
 
-        def quantize_h(c, a):
-            j0, j1 = CHUNKS[c]
-            nc.vector.quantize_mx(
-                out=h_codes[a][:, j0:j1].bitcast(FP8X4), scales=h_scales[a][:, j0:j1], in_=h_bf[c, a][:]
-            )
+        spent = {}
+        h2_words = h_bf[2][:].bitcast(F32)
+        spent["h2", 0], spent["h2", 1] = h2_words[:, :512], h2_words[:, 512:]
+        spent["h2", 2], spent["h2", 3] = h2_words[:, 512:768], h2_words[:, 768:]
 
-        moved = {}
+        negated, late_from = {}, {}
 
-        def gather_move(i, j0, j1):
-            width = j1 - j0
-            y = y_psum.tile([P, width], F32, name="y")
-            for a in range(PASSES):
-                cols = slice(K * a + P * i, K * a + P * (i + 1))
+        def predict_late(a, j0):
+            for t in range(PACK):
+                pred = turn_psum.tile([P, S - j0], F32, name="turn")
                 nc.tensor.matmul_mx(
-                    out=y[:],
-                    lhsT=b_words[:, cols].bitcast(FP8X4),
-                    lhsT_scale=b_scales[:, cols],
-                    rhs=h_codes[a][:, j0:j1].bitcast(FP8X4),
-                    rhs_scale=h_scales[a][:, j0:j1],
-                    start=(a == 0),
-                    stop=(a == PASSES - 1),
+                    out=pred[:],
+                    lhsT=gm_codes[a][:, P * t : P * (t + 1)].bitcast(FP8X4),
+                    lhsT_scale=gm_scales[a][:, P * t : P * (t + 1)],
+                    rhs=v_words[:, j0:S].bitcast(FP8X4),
+                    rhs_scale=v_scales[:, j0:S],
+                    start=True,
+                    stop=True,
                 )
-            scaled = sb("scaled%d_%d" % (i, j0), [P, width], F32)
-            nc.scalar.activation(scaled[:], y[:], ACT.Copy, scale=steps[:, i : i + 1])
-            summed = sb("summed%d_%d" % (i, j0), [P, width], F32)
-            nc.vector.tensor_tensor(
-                summed[:], maps[i][:].indirect(offsets[:, j0 // 16 : j1 // 16]), scaled[:], ALU.add
-            )
-            new = sb("new%d_%d" % (i, j0), [P, width], F32)
-            nc.scalar.activation(new[:], summed[:], ACT.Relu)
-            moved[i, j0] = new
+                negated[a, t] = field_tiles[0, a][:, t, j0 - 512 :]
+                late_from[a] = j0
+                nc.scalar.activation(negated[a, t][:], pred[:], ACT.Copy, scale=-1.0)
 
-        def scatter(i, j0, j1):
-            nc.vector.tensor_copy(maps[i][:].indirect(offsets[:, j0 // 16 : j1 // 16]), moved[i, j0][:])
+        def residual_by_transposes(c, a):
+            j0, j1 = CHUNKS[c]
+            width = j1 - j0
+            for pair in range(width // (2 * P)):
+                rounded = sb("h_turned%d_%d_%d" % (c, a, pair), [P, PASS], F32)
+                spent[c, a] = rounded
+                for b in (2 * pair, 2 * pair + 1):
+                    cols = slice(P * b, P * (b + 1))
+                    turned = turn_psum.tile([P, PACK, P], F32, name="turn")
+                    for t in range(PACK):
+                        nc.tensor.matmul(
+                            turned[:, t, :], fields[c, a][:, t, cols], identity[:],
+                            start=True, stop=False, is_transpose=True,
+                        )
+                        nc.tensor.matmul(
+                            turned[:, t, :], negated[a, t][:, j0 - late_from[a] + P * b : j0 - late_from[a] + P * (b + 1)], identity[:],
+                            start=False, stop=True, is_transpose=True,
+                        )
+                    h_turned = rounded[:, 2 * P * (b % 2) : 2 * P * (b % 2 + 1)]
+                    nc.scalar.activation(
+                        h_turned.bitcast(BF16).rearrange("j (u p e) -> j u p e", u=2, e=2),
+                        turned[:].rearrange("j (u e) p -> j u p e", u=2),
+                        ACT.Copy,
+                    )
+                back_turned = turn_psum.tile([P, 2, 2, P], F32, name="turn")
+                for n in range(2):
+                    for u in range(2):
+                        nc.tensor.transpose(
+                            back_turned[:, n, u, :], rounded[:, P * (2 * n + u) : P * (2 * n + u + 1)], identity[:]
+                        )
+                at = 2 * (width * a + 2 * P * pair)
+                nc.scalar.copy(
+                    h_bf[c][:].bitcast(F32)[:, at : at + PASS].rearrange("p (n j u) -> p n j u", n=2, u=2),
+                    back_turned[:].rearrange("p n u j -> p n j u"),
+                )
+
+        def quantize_h(c):
+            nc.vector.quantize_mx(out=h_codes[c][:].bitcast(FP8X4), scales=h_scales[c][:], in_=h_bf[c][:])
+
+        scaled, moved = {}, {}
+
+        def lead_back(i, first, last):
+            j0, j1 = CHUNKS[first][0], CHUNKS[last][1]
+            y = y_psum.tile([P, j1 - j0], F32, name="y")
+            for c in range(last, first - 1, -1):
+                c0, c1 = CHUNKS[c]
+                for a in range(PASSES):
+                    cols = slice(K * a + P * i, K * a + P * (i + 1))
+                    part = slice((c1 - c0) * a, (c1 - c0) * (a + 1))
+                    nc.tensor.matmul_mx(
+                        out=y[:, c0 - j0 : c1 - j0],
+                        lhsT=b_words[:, cols].bitcast(FP8X4),
+                        lhsT_scale=b_scales[:, cols],
+                        rhs=h_codes[c][:, part].bitcast(FP8X4),
+                        rhs_scale=h_scales[c][:, part],
+                        start=(a == 0),
+                        stop=(a == PASSES - 1),
+                    )
+            both = sb("scaled%d_%d" % (i, first), [P, j1 - j0], F32)
+            nc.scalar.activation(both[:], y[:], ACT.Copy, scale=steps[:, i : i + 1])
+            for c in range(first, last + 1):
+                scaled[i, c] = both[:, CHUNKS[c][0] - j0 :]
+
+        def gather_move(i, first, last, into=None, sum_into=None):
+            j0, j1 = CHUNKS[first][0], CHUNKS[last][1]
+            summed = spent[sum_into] if sum_into else sb("summed%d_%d" % (i, first), [P, j1 - j0], F32)
+            spent["sum", i, first] = summed
+            nc.vector.tensor_tensor(
+                summed[:], maps[i][:].indirect(offsets[:, j0 // 16 : j1 // 16]), scaled[i, first][:, : j1 - j0], ALU.add
+            )
+            if into != "later":
+                clamp(i, first, last, into)
+
+        def clamp(i, first, last, into):
+            j0, j1 = CHUNKS[first][0], CHUNKS[last][1]
+            summed = spent["sum", i, first]
+            moved[i, first] = spent[into][:, spent[into].shape[1] - (j1 - j0) :] if into else sb("new%d_%d" % (i, first), [P, j1 - j0], F32)
+            nc.scalar.activation(moved[i, first][:], summed[:], ACT.Relu)
+
+        def scatter(i, first, last):
+            j0, j1 = CHUNKS[first][0], CHUNKS[last][1]
+            nc.vector.tensor_copy(maps[i][:].indirect(offsets[:, j0 // 16 : j1 // 16]), moved[i, first][:])
             if j1 == S:
                 nc.sync.dma_start(out[P * i : P * (i + 1), :], maps[i][:])
 
         weave_gm(0)
-        weave_gm(1)
         quantize_gm(0)
-        weave_gm(2)
-        weave_gm(3)
+        weave_gm(1)
         quantize_gm(1)
         residual(0, 0)
-        residual(0, 1)
-        quantize_h(0, 0)
-        quantize_h(0, 1)
-        gather_move(0, 0, 256)
         residual(1, 0)
-        scatter(0, 0, 256)
+        residual(0, 1)
+        quantize_h(0)
         residual(1, 1)
-        gather_move(1, 0, 256)
-        quantize_h(1, 0)
-        quantize_h(1, 1)
-        scatter(1, 0, 256)
-        gather_move(0, 256, 512)
-        gather_move(1, 256, 512)
-        scatter(0, 256, 512)
-        gather_move(2, 0, 512)
-        scatter(1, 256, 512)
-        residual(2, 0)
-        scatter(2, 0, 512)
-        gather_move(3, 0, 512)
+        quantize_h(1)
+        lead_back(0, 0, 0)
+        lead_back(1, 0, 0)
+        lead_back(0, 1, 1)
+        lead_back(1, 1, 1)
+        gather_move(0, 0, 0)
+        gather_move(1, 0, 0)
+        gather_move(0, 1, 1, ("h2", 2))
+        gather_move(1, 1, 1, ("h2", 3))
+        scatter(0, 0, 0)
+        scatter(1, 0, 0)
+        scatter(0, 1, 1)
+        scatter(1, 1, 1)
+        predict_late(0, 512)
+        residual_by_transposes(2, 0)
+        lead_back(2, 0, 1)
+        lead_back(3, 0, 1)
+        predict_late(1, 768)
+        gather_move(2, 0, 1, "later")
         residual(2, 1)
-        quantize_h(2, 0)
-        quantize_h(2, 1)
-        scatter(3, 0, 512)
-        gather_move(0, 512, 1024)
-        for i in range(TILES):
-            if i + 1 < TILES:
-                gather_move(i + 1, 512, 1024)
-            scatter(i, 512, 1024)
+        quantize_h(2)
+        clamp(2, 0, 1, ("h2", 0))
+        gather_move(3, 0, 1, ("sum", 2, 0), ("h2", 1))
+        scatter(2, 0, 1)
+        scatter(3, 0, 1)
+        residual_by_transposes(3, 0)
+        residual_by_transposes(3, 1)
+        quantize_h(3)
+        lead_back(0, 2, 2)
+        lead_back(1, 2, 2)
+        gather_move(0, 2, 2, (3, 1))
+        gather_move(1, 2, 2, ("sum", 0, 2))
+        scatter(0, 2, 2)
+        scatter(1, 2, 2)
+        lead_back(0, 3, 3)
+        lead_back(1, 3, 3)
+        lead_back(2, 2, 3)
+        lead_back(3, 2, 3)
+        gather_move(0, 3, 3)
+        gather_move(1, 3, 3)
+        gather_move(2, 2, 3)
+        gather_move(3, 2, 3)
+        scatter(0, 3, 3)
+        scatter(1, 3, 3)
+        scatter(2, 2, 3)
+        scatter(3, 2, 3)

@@ -21,8 +21,11 @@ PACK = 4
 PASS = P * PACK
 PASSES = H // PASS
 TILES = K // P
-SCALAR_SHARE = 44
-CHUNKS = ((0, 256), (256, 512), (512, 768), (768, 1024))
+CHUNK = 256
+CHUNKS = S // CHUNK
+HALF = 2 * CHUNK
+QUADS = 4
+SCALAR_SHARE = 28
 
 
 def tile_list_villa_survey_step_kernel(
@@ -35,14 +38,14 @@ def tile_list_villa_survey_step_kernel(
         turn_psum = ctx.enter_context(tc.psum_pool(name="turn_psum", bufs=3))
         y_psum = ctx.enter_context(tc.psum_pool(name="y_psum", bufs=2))
 
-        def sb(name, shape, dtype, tag=None):
-            return keep.tile(shape, dtype, name=name, tag=tag or name, align_bytes=64)
+        def sb(name, shape, dtype):
+            return keep.tile(shape, dtype, name=name, tag=name, align_bytes=64)
 
         offsets = keep.tile([P, S // 16], U16, name="offsets")
         table_scales = sb("table_scales", [P, T], U8)
         table_words = sb("table_words", [P, T], I32)
         b_scales = sb("b_scales", [P, PASSES * K], U8)
-        b_words = sb("b_words", [P, PASSES * K], I32)
+        b_words = [sb("b_words%d" % n, [P, PASSES * 2 * P], I32) for n in range(TILES // 2)]
         steps = sb("steps", [P, TILES], F32)
         maps = [sb("map%d" % i, [P, T], F32) for i in range(TILES)]
         gm_raw = [sb("gm_raw%d" % a, [P, PACK, PASS], F32) for a in range(PASSES)]
@@ -52,79 +55,65 @@ def tile_list_villa_survey_step_kernel(
         v_words = sb("v_words", [P, S], U32)
         v_scales = sb("v_scales", [P, S], U8)
         identity = sb("identity", [P, P], F32)
-        fields = {}
         h_bf, h_codes, h_scales = [], [], []
-        for c, (j0, j1) in enumerate(CHUNKS):
-            h_bf.append(sb("h_bf%d" % c, [P, PASSES * (j1 - j0) * PACK], BF16))
-            h_codes.append(sb("h_codes%d" % c, [P, PASSES * (j1 - j0)], U32))
-            h_scales.append(sb("h_scales%d" % c, [P, PASSES * (j1 - j0)], U8))
-        field_tiles = {}
-        for half in range(2):
+        for c in range(CHUNKS):
+            h_bf.append(sb("h_bf%d" % c, [P, PASSES * CHUNK * PACK], BF16))
+            h_codes.append(sb("h_codes%d" % c, [P, PASSES * CHUNK], U32))
+            h_scales.append(sb("h_scales%d" % c, [P, PASSES * CHUNK], U8))
+        field_halves = {}
+        for half in range(S // HALF):
             for a in range(PASSES):
-                field_tiles[half, a] = sb("field%d_%d" % (half, a), [P, PACK, 512], F32)
-                for c in (2 * half, 2 * half + 1):
-                    fields[c, a] = field_tiles[half, a][:, :, 256 * (c % 2) : 256 * (c % 2 + 1)]
+                field_halves[half, a] = sb("field%d_%d" % (half, a), [P, PACK, HALF], F32)
+        step_rows = sb("step_rows", [P, P], F32)
+        summed2 = sb("summed2", [P, HALF], F32)
 
         nc.gpsimd.memset(table_scales[:].bitcast(I32), 0)
         nc.vector.memset(b_scales[:].bitcast(I32), 0)
         make_identity(nc, identity[:])
-        step_rows = sb("step_rows", [P, P], F32)
         nc.gpsimd.memset(step_rows[:], 0.0)
 
-        def load_gm(a, lo=0, hi=PASS):
-            columns = gm[:, PASS * a + lo : PASS * a + hi]
-            nc.sync.dma_start(gm_raw[a][:, :, lo:hi], columns.rearrange("(p j) c -> p j c", j=PACK))
+        def load_gm(a):
+            columns = gm[:, PASS * a : PASS * (a + 1)]
+            nc.sync.dma_start(gm_raw[a][:], columns.rearrange("(p j) c -> p j c", j=PACK))
 
-        def load_field(half, a, lo=0, hi=512):
-            rows = field[PASS * a : PASS * (a + 1), 512 * half + lo : 512 * half + hi]
-            nc.sync.dma_start(field_tiles[half, a][:, :, lo:hi], rows.rearrange("(p t) j -> p t j", t=PACK))
+        def load_field(half, a):
+            rows = field[PASS * a : PASS * (a + 1), HALF * half : HALF * (half + 1)]
+            nc.sync.dma_start(field_halves[half, a][:], rows.rearrange("(p t) j -> p t j", t=PACK))
 
-        def load_step():
-            nc.sync.dma_start(step_rows[:TILES, :], step.rearrange("(i p) -> i p", p=P))
-            step_turned = turn_psum.tile([P, P], F32, name="turn")
-            nc.tensor.transpose(step_turned[:], step_rows[:], identity[:])
-            nc.scalar.copy(steps[:], step_turned[:, :TILES])
-
-        def load_table_scales():
-            for quad in range(4):
-                nc.sync.dma_start(
-                    table_scales[32 * quad : 32 * quad + 4, :].bitcast(I32),
-                    tab_scales[0, 4 * quad : 4 * quad + 4, :].bitcast(I32),
-                )
-
-        def load_table_words():
-            nc.sync.dma_start(table_words[:], tab_words[0].rearrange("p t i -> p (t i)").bitcast(I32))
-
-        def load_back_scales():
-            for quad in range(4):
-                nc.sync.dma_start(
-                    b_scales[32 * quad : 32 * quad + 4, :].bitcast(I32).rearrange("r (a c) -> r a c", a=PASSES),
-                    back_scales[:, 4 * quad : 4 * quad + 4, :].bitcast(I32).rearrange("a r c -> r a c"),
-                )
-
-        def load_back_words(lo=0, hi=K):
+        def load_back_words(n):
             nc.sync.dma_start(
-                b_words[:].rearrange("p (a c) -> p a c", a=PASSES)[:, :, lo:hi],
-                back_words.rearrange("a p c i -> p a (c i)").bitcast(I32)[:, :, lo:hi],
+                b_words[n][:].rearrange("p (a c) -> p a c", a=PASSES),
+                back_words.rearrange("a p c i -> p a (c i)").bitcast(I32)[:, :, 2 * P * n : 2 * P * (n + 1)],
             )
 
         def load_map(i):
             nc.sync.dma_start(maps[i][:], gT[P * i : P * (i + 1), :])
 
         nc.sync.dma_start(offsets[:], offs)
-        load_table_words()
-        load_table_scales()
+        nc.sync.dma_start(table_words[:], tab_words[0].rearrange("p t i -> p (t i)").bitcast(I32))
+        for quad in range(QUADS):
+            nc.sync.dma_start(
+                table_scales[32 * quad : 32 * quad + 4, :].bitcast(I32),
+                tab_scales[0, 4 * quad : 4 * quad + 4, :].bitcast(I32),
+            )
         load_gm(0)
         load_gm(1)
-        load_step()
+        nc.sync.dma_start(step_rows[:TILES, :], step.rearrange("(i p) -> i p", p=P))
+        step_turned = turn_psum.tile([P, P], F32, name="turn")
+        nc.tensor.transpose(step_turned[:], step_rows[:], identity[:])
+        nc.scalar.copy(steps[:], step_turned[:, :TILES])
         load_field(0, 0)
         load_field(0, 1)
-        load_back_scales()
-        load_back_words(0, 256)
+        for quad in range(QUADS):
+            nc.sync.dma_start(
+                b_scales[32 * quad : 32 * quad + 4, :].bitcast(I32).rearrange("r (a c) -> r a c", a=PASSES),
+                back_scales[:, 4 * quad : 4 * quad + 4, :].bitcast(I32).rearrange("a r c -> r a c"),
+            )
+        load_back_words(0)
         load_map(0)
         load_map(1)
-        load_back_words(256, 512)
         load_field(1, 0)
+        load_back_words(1)
         load_map(2)
         load_field(1, 1)
         load_map(3)
@@ -132,195 +121,182 @@ def tile_list_villa_survey_step_kernel(
         nc.vector.tensor_copy(v_scales[:], table_scales[:].indirect(offsets[:]))
         nc.vector.tensor_copy(v_words[:], table_words[:].bitcast(U32).indirect(offsets[:]))
 
-        def weave_gm(a):
+        def quantize_gm(a):
             dst = gm_bf[a][:].rearrange("p (t m j) -> p m j t", t=PACK, j=PACK)
             src = gm_raw[a][:].rearrange("p j (m t) -> p m j t", t=PACK)
             nc.scalar.copy(dst[:, :SCALAR_SHARE], src[:, :SCALAR_SHARE])
             nc.vector.tensor_copy(dst[:, SCALAR_SHARE:], src[:, SCALAR_SHARE:])
-
-        def quantize_gm(a):
             nc.vector.quantize_mx(out=gm_codes[a][:].bitcast(FP8X4), scales=gm_scales[a][:], in_=gm_bf[a][:])
 
-        def residual(c, a):
-            j0, j1 = CHUNKS[c]
-            for b in range((j1 - j0) // P):
-                cols = slice(j0 + P * b, j0 + P * (b + 1))
+        def predict(dst, a, t, entries):
+            nc.tensor.matmul_mx(
+                out=dst,
+                lhsT=gm_codes[a][:, P * t : P * (t + 1)].bitcast(FP8X4),
+                lhsT_scale=gm_scales[a][:, P * t : P * (t + 1)],
+                rhs=v_words[:, entries].bitcast(FP8X4),
+                rhs_scale=v_scales[:, entries],
+                start=True,
+                stop=True,
+            )
+
+        def measured(c, a, b):
+            first = CHUNK * (c % 2) + P * b
+            return field_halves[c // 2, a][:, :, first : first + P]
+
+        def residual_on_vector(c, a):
+            for b in range(CHUNK // P):
                 pred = pred_psum.tile([P, PACK, P], F32, name="pred")
                 for t in range(PACK):
-                    nc.tensor.matmul_mx(
-                        out=pred[:, t, :],
-                        lhsT=gm_codes[a][:, P * t : P * (t + 1)].bitcast(FP8X4),
-                        lhsT_scale=gm_scales[a][:, P * t : P * (t + 1)],
-                        rhs=v_words[:, cols].bitcast(FP8X4),
-                        rhs_scale=v_scales[:, cols],
-                        start=True,
-                        stop=True,
-                    )
-                at = PACK * ((j1 - j0) * a + P * b)
-                dst = h_bf[c][:, at : at + PASS].rearrange("p (g i t) -> p g t i", i=2, t=PACK)
-                measured = fields[c, a][:, :, P * b : P * (b + 1)].rearrange("p t (g i) -> p g t i", i=2)
-                nc.vector.tensor_tensor(dst, measured, pred[:].rearrange("p t (g i) -> p g t i", i=2), ALU.subtract)
-
-        spent = {}
-        h2_words = h_bf[2][:].bitcast(F32)
-        spent["h2", 0], spent["h2", 1] = h2_words[:, :512], h2_words[:, 512:]
-        spent["h2", 2], spent["h2", 3] = h2_words[:, 512:768], h2_words[:, 768:]
-
-        negated, late_from = {}, {}
-
-        def predict_late(a, j0):
-            for t in range(PACK):
-                pred = turn_psum.tile([P, S - j0], F32, name="turn")
-                nc.tensor.matmul_mx(
-                    out=pred[:],
-                    lhsT=gm_codes[a][:, P * t : P * (t + 1)].bitcast(FP8X4),
-                    lhsT_scale=gm_scales[a][:, P * t : P * (t + 1)],
-                    rhs=v_words[:, j0:S].bitcast(FP8X4),
-                    rhs_scale=v_scales[:, j0:S],
-                    start=True,
-                    stop=True,
+                    predict(pred[:, t, :], a, t, slice(CHUNK * c + P * b, CHUNK * c + P * (b + 1)))
+                at = PACK * (CHUNK * a + P * b)
+                nc.vector.tensor_tensor(
+                    h_bf[c][:, at : at + PASS].rearrange("p (g i t) -> p g t i", i=2, t=PACK),
+                    measured(c, a, b).rearrange("p t (g i) -> p g t i", i=2),
+                    pred[:].rearrange("p t (g i) -> p g t i", i=2),
+                    ALU.subtract,
                 )
-                negated[a, t] = field_tiles[0, a][:, t, j0 - 512 :]
-                late_from[a] = j0
-                nc.scalar.activation(negated[a, t][:], pred[:], ACT.Copy, scale=-1.0)
+
+        def negate_predictions(a, first_chunk):
+            first = CHUNK * first_chunk
+            for t in range(PACK):
+                pred = turn_psum.tile([P, S - first], F32, name="turn")
+                predict(pred[:], a, t, slice(first, S))
+                nc.scalar.activation(field_halves[0, a][:, t, first - HALF :], pred[:], ACT.Copy, scale=-1.0)
 
         def residual_by_transposes(c, a):
-            j0, j1 = CHUNKS[c]
-            width = j1 - j0
-            for pair in range(width // (2 * P)):
-                rounded = sb("h_turned%d_%d_%d" % (c, a, pair), [P, PASS], F32)
-                spent[c, a] = rounded
-                for b in (2 * pair, 2 * pair + 1):
-                    cols = slice(P * b, P * (b + 1))
-                    turned = turn_psum.tile([P, PACK, P], F32, name="turn")
-                    for t in range(PACK):
-                        nc.tensor.matmul(
-                            turned[:, t, :], fields[c, a][:, t, cols], identity[:],
-                            start=True, stop=False, is_transpose=True,
-                        )
-                        nc.tensor.matmul(
-                            turned[:, t, :], negated[a, t][:, j0 - late_from[a] + P * b : j0 - late_from[a] + P * (b + 1)], identity[:],
-                            start=False, stop=True, is_transpose=True,
-                        )
-                    h_turned = rounded[:, 2 * P * (b % 2) : 2 * P * (b % 2 + 1)]
-                    nc.scalar.activation(
-                        h_turned.bitcast(BF16).rearrange("j (u p e) -> j u p e", u=2, e=2),
-                        turned[:].rearrange("j (u e) p -> j u p e", u=2),
-                        ACT.Copy,
+            negated = field_halves[0, a]
+            rounded = sb("rounded%d_%d" % (c, a), [P, PASS], F32)
+            for b in range(CHUNK // P):
+                first = CHUNK * (c % 2) + P * b
+                turned = turn_psum.tile([P, PACK, P], F32, name="turn")
+                for t in range(PACK):
+                    nc.tensor.matmul(
+                        turned[:, t, :], measured(c, a, b)[:, t, :], identity[:],
+                        start=True, stop=False, is_transpose=True,
                     )
-                back_turned = turn_psum.tile([P, 2, 2, P], F32, name="turn")
-                for n in range(2):
-                    for u in range(2):
-                        nc.tensor.transpose(
-                            back_turned[:, n, u, :], rounded[:, P * (2 * n + u) : P * (2 * n + u + 1)], identity[:]
-                        )
-                at = 2 * (width * a + 2 * P * pair)
-                nc.scalar.copy(
-                    h_bf[c][:].bitcast(F32)[:, at : at + PASS].rearrange("p (n j u) -> p n j u", n=2, u=2),
-                    back_turned[:].rearrange("p n u j -> p n j u"),
+                    nc.tensor.matmul(
+                        turned[:, t, :], negated[:, t, first : first + P], identity[:],
+                        start=False, stop=True, is_transpose=True,
+                    )
+                nc.scalar.activation(
+                    rounded[:, 2 * P * b : 2 * P * (b + 1)].bitcast(BF16).rearrange("j (u p e) -> j u p e", u=2, e=2),
+                    turned[:].rearrange("j (u e) p -> j u p e", u=2),
+                    ACT.Copy,
                 )
+            pairs = turn_psum.tile([P, 2, 2, P], F32, name="turn")
+            for b in range(CHUNK // P):
+                for u in range(2):
+                    nc.tensor.transpose(pairs[:, b, u, :], rounded[:, P * (2 * b + u) : P * (2 * b + u + 1)], identity[:])
+            nc.scalar.copy(
+                h_bf[c][:].bitcast(F32)[:, PASS * a : PASS * (a + 1)].rearrange("p (b j u) -> p b j u", b=2, u=2),
+                pairs[:].rearrange("p b u j -> p b j u"),
+            )
+            return rounded
 
         def quantize_h(c):
             nc.vector.quantize_mx(out=h_codes[c][:].bitcast(FP8X4), scales=h_scales[c][:], in_=h_bf[c][:])
 
-        scaled, moved = {}, {}
+        scaled, summed, new = {}, {}, {}
 
-        def lead_back(i, first, last):
-            j0, j1 = CHUNKS[first][0], CHUNKS[last][1]
-            y = y_psum.tile([P, j1 - j0], F32, name="y")
+        def width(piece):
+            return CHUNK * (piece[2] + 1 - piece[1])
+
+        def window(piece):
+            i, first, last = piece
+            return maps[i][:].indirect(offsets[:, CHUNK * first // 16 : CHUNK * (last + 1) // 16])
+
+        def lead_back(piece):
+            i, first, last = piece
+            y = y_psum.tile([P, width(piece)], F32, name="y")
             for c in range(last, first - 1, -1):
-                c0, c1 = CHUNKS[c]
                 for a in range(PASSES):
-                    cols = slice(K * a + P * i, K * a + P * (i + 1))
-                    part = slice((c1 - c0) * a, (c1 - c0) * (a + 1))
+                    word = 2 * P * a + P * (i % 2)
                     nc.tensor.matmul_mx(
-                        out=y[:, c0 - j0 : c1 - j0],
-                        lhsT=b_words[:, cols].bitcast(FP8X4),
-                        lhsT_scale=b_scales[:, cols],
-                        rhs=h_codes[c][:, part].bitcast(FP8X4),
-                        rhs_scale=h_scales[c][:, part],
+                        out=y[:, CHUNK * (c - first) : CHUNK * (c - first + 1)],
+                        lhsT=b_words[i // 2][:, word : word + P].bitcast(FP8X4),
+                        lhsT_scale=b_scales[:, K * a + P * i : K * a + P * (i + 1)],
+                        rhs=h_codes[c][:, CHUNK * a : CHUNK * (a + 1)].bitcast(FP8X4),
+                        rhs_scale=h_scales[c][:, CHUNK * a : CHUNK * (a + 1)],
                         start=(a == 0),
                         stop=(a == PASSES - 1),
                     )
-            both = sb("scaled%d_%d" % (i, first), [P, j1 - j0], F32)
-            nc.scalar.activation(both[:], y[:], ACT.Copy, scale=steps[:, i : i + 1])
-            for c in range(first, last + 1):
-                scaled[i, c] = both[:, CHUNKS[c][0] - j0 :]
+            scaled[piece] = sb("scaled%d_%d" % piece[:2], [P, width(piece)], F32)
+            nc.scalar.activation(scaled[piece][:], y[:], ACT.Copy, scale=steps[:, i : i + 1])
 
-        def gather_move(i, first, last, into=None, sum_into=None):
-            j0, j1 = CHUNKS[first][0], CHUNKS[last][1]
-            summed = spent[sum_into] if sum_into else sb("summed%d_%d" % (i, first), [P, j1 - j0], F32)
-            spent["sum", i, first] = summed
-            nc.vector.tensor_tensor(
-                summed[:], maps[i][:].indirect(offsets[:, j0 // 16 : j1 // 16]), scaled[i, first][:, : j1 - j0], ALU.add
-            )
-            if into != "later":
-                clamp(i, first, last, into)
+        def own(kind, piece):
+            return sb("%s%d_%d" % (kind, piece[0], piece[1]), [P, width(piece)], F32)[:]
 
-        def clamp(i, first, last, into):
-            j0, j1 = CHUNKS[first][0], CHUNKS[last][1]
-            summed = spent["sum", i, first]
-            moved[i, first] = spent[into][:, spent[into].shape[1] - (j1 - j0) :] if into else sb("new%d_%d" % (i, first), [P, j1 - j0], F32)
-            nc.scalar.activation(moved[i, first][:], summed[:], ACT.Relu)
+        def gather_add(piece, dst):
+            summed[piece] = dst
+            nc.vector.tensor_tensor(dst, window(piece), scaled[piece][:], ALU.add)
 
-        def scatter(i, first, last):
-            j0, j1 = CHUNKS[first][0], CHUNKS[last][1]
-            nc.vector.tensor_copy(maps[i][:].indirect(offsets[:, j0 // 16 : j1 // 16]), moved[i, first][:])
-            if j1 == S:
+        def clamp(piece, dst):
+            new[piece] = dst
+            nc.scalar.activation(dst, summed[piece], ACT.Relu)
+
+        def move(piece):
+            gather_add(piece, own("summed", piece))
+            clamp(piece, own("new", piece))
+
+        def scatter(piece):
+            i, first, last = piece
+            nc.vector.tensor_copy(window(piece), new[piece])
+            if last == CHUNKS - 1:
                 nc.sync.dma_start(out[P * i : P * (i + 1), :], maps[i][:])
 
-        weave_gm(0)
-        quantize_gm(0)
-        weave_gm(1)
-        quantize_gm(1)
-        residual(0, 0)
-        residual(1, 0)
-        residual(0, 1)
+        h2_words = h_bf[2][:].bitcast(F32)
+
+        for a in range(PASSES):
+            quantize_gm(a)
+        residual_on_vector(0, 0)
+        residual_on_vector(1, 0)
+        residual_on_vector(0, 1)
         quantize_h(0)
-        residual(1, 1)
+        residual_on_vector(1, 1)
         quantize_h(1)
-        lead_back(0, 0, 0)
-        lead_back(1, 0, 0)
-        lead_back(0, 1, 1)
-        lead_back(1, 1, 1)
-        gather_move(0, 0, 0)
-        gather_move(1, 0, 0)
-        gather_move(0, 1, 1, ("h2", 2))
-        gather_move(1, 1, 1, ("h2", 3))
-        scatter(0, 0, 0)
-        scatter(1, 0, 0)
-        scatter(0, 1, 1)
-        scatter(1, 1, 1)
-        predict_late(0, 512)
+
+        early = [(i, c, c) for c in range(2) for i in range(2)]
+        for piece in early:
+            lead_back(piece)
+        move((0, 0, 0))
+        move((1, 0, 0))
+        gather_add((0, 1, 1), own("summed", (0, 1, 1)))
+        clamp((0, 1, 1), summed2[:, :CHUNK])
+        gather_add((1, 1, 1), own("summed", (1, 1, 1)))
+        clamp((1, 1, 1), h2_words[:, PASS + P : PASS + P + CHUNK])
+        for piece in early:
+            scatter(piece)
+
+        negate_predictions(0, 2)
         residual_by_transposes(2, 0)
-        lead_back(2, 0, 1)
-        lead_back(3, 0, 1)
-        predict_late(1, 768)
-        gather_move(2, 0, 1, "later")
-        residual(2, 1)
+        lead_back((2, 0, 1))
+        lead_back((3, 0, 1))
+        negate_predictions(1, 3)
+        gather_add((2, 0, 1), summed2[:])
+        residual_on_vector(2, 1)
         quantize_h(2)
-        clamp(2, 0, 1, ("h2", 0))
-        gather_move(3, 0, 1, ("sum", 2, 0), ("h2", 1))
-        scatter(2, 0, 1)
-        scatter(3, 0, 1)
+        clamp((2, 0, 1), h2_words[:, :PASS])
+        gather_add((3, 0, 1), h2_words[:, PASS:])
+        clamp((3, 0, 1), summed2[:])
+        scatter((2, 0, 1))
+        scatter((3, 0, 1))
+
         residual_by_transposes(3, 0)
-        residual_by_transposes(3, 1)
+        last_rounded = residual_by_transposes(3, 1)
         quantize_h(3)
-        lead_back(0, 2, 2)
-        lead_back(1, 2, 2)
-        gather_move(0, 2, 2, (3, 1))
-        gather_move(1, 2, 2, ("sum", 0, 2))
-        scatter(0, 2, 2)
-        scatter(1, 2, 2)
-        lead_back(0, 3, 3)
-        lead_back(1, 3, 3)
-        lead_back(2, 2, 3)
-        lead_back(3, 2, 3)
-        gather_move(0, 3, 3)
-        gather_move(1, 3, 3)
-        gather_move(2, 2, 3)
-        gather_move(3, 2, 3)
-        scatter(0, 3, 3)
-        scatter(1, 3, 3)
-        scatter(2, 2, 3)
-        scatter(3, 2, 3)
+        lead_back((0, 2, 2))
+        lead_back((1, 2, 2))
+        gather_add((0, 2, 2), own("summed", (0, 2, 2)))
+        clamp((0, 2, 2), last_rounded[:, CHUNK:])
+        gather_add((1, 2, 2), own("summed", (1, 2, 2)))
+        clamp((1, 2, 2), summed[0, 2, 2])
+        scatter((0, 2, 2))
+        scatter((1, 2, 2))
+
+        late = [(0, 3, 3), (1, 3, 3), (2, 2, 3), (3, 2, 3)]
+        for piece in late:
+            lead_back(piece)
+        for piece in late:
+            move(piece)
+        for piece in late:
+            scatter(piece)

@@ -25,7 +25,7 @@ CHUNK = 256
 CHUNKS = S // CHUNK
 HALF = 2 * CHUNK
 QUADS = 4
-SCALAR_SHARE = 28
+SCALAR_SHARE = (64, 36)
 
 
 def tile_list_villa_survey_step_kernel(
@@ -49,7 +49,8 @@ def tile_list_villa_survey_step_kernel(
         steps = sb("steps", [P, TILES], F32)
         maps = [sb("map%d" % i, [P, T], F32) for i in range(TILES)]
         gm_raw = [sb("gm_raw%d" % a, [P, PACK, PASS], F32) for a in range(PASSES)]
-        gm_bf = [sb("gm_bf%d" % a, [P, PASS * PACK], BF16) for a in range(PASSES)]
+        woven = sb("woven", [P, PASS * PACK], BF16)
+        gm_bf = [woven, woven]
         gm_codes = [sb("gm_codes%d" % a, [P, PASS], U32) for a in range(PASSES)]
         gm_scales = [sb("gm_scales%d" % a, [P, PASS], U8) for a in range(PASSES)]
         v_words = sb("v_words", [P, S], U32)
@@ -59,7 +60,7 @@ def tile_list_villa_survey_step_kernel(
         for c in range(CHUNKS):
             h_bf.append(sb("h_bf%d" % c, [P, PASSES * CHUNK * PACK], BF16))
             h_codes.append(sb("h_codes%d" % c, [P, PASSES * CHUNK], U32))
-            h_scales.append(sb("h_scales%d" % c, [P, PASSES * CHUNK], U8))
+            h_scales.append(None if c == 1 else sb("h_scales%d" % c, [P, PASSES * CHUNK], U8))
         field_halves = {}
         for half in range(S // HALF):
             for a in range(PASSES):
@@ -69,8 +70,8 @@ def tile_list_villa_survey_step_kernel(
 
         nc.gpsimd.memset(table_scales[:].bitcast(I32), 0)
         nc.vector.memset(b_scales[:].bitcast(I32), 0)
-        make_identity(nc, identity[:])
         nc.gpsimd.memset(step_rows[:], 0.0)
+        make_identity(nc, identity[:])
 
         def load_gm(a):
             columns = gm[:, PASS * a : PASS * (a + 1)]
@@ -90,18 +91,20 @@ def tile_list_villa_survey_step_kernel(
             nc.sync.dma_start(maps[i][:], gT[P * i : P * (i + 1), :])
 
         nc.sync.dma_start(offsets[:], offs)
-        nc.sync.dma_start(table_words[:], tab_words[0].rearrange("p t i -> p (t i)").bitcast(I32))
+        words = tab_words[0].rearrange("p t i -> p (t i)").bitcast(I32)
+        nc.sync.dma_start(table_words[:, :PASS], words[:, :PASS])
         for quad in range(QUADS):
             nc.sync.dma_start(
                 table_scales[32 * quad : 32 * quad + 4, :].bitcast(I32),
                 tab_scales[0, 4 * quad : 4 * quad + 4, :].bitcast(I32),
             )
-        load_gm(0)
-        load_gm(1)
+        nc.sync.dma_start(table_words[:, PASS:], words[:, PASS:])
         nc.sync.dma_start(step_rows[:TILES, :], step.rearrange("(i p) -> i p", p=P))
         step_turned = turn_psum.tile([P, P], F32, name="turn")
         nc.tensor.transpose(step_turned[:], step_rows[:], identity[:])
         nc.scalar.copy(steps[:], step_turned[:, :TILES])
+        load_gm(0)
+        load_gm(1)
         load_field(0, 0)
         load_field(0, 1)
         for quad in range(QUADS):
@@ -124,8 +127,8 @@ def tile_list_villa_survey_step_kernel(
         def quantize_gm(a):
             dst = gm_bf[a][:].rearrange("p (t m j) -> p m j t", t=PACK, j=PACK)
             src = gm_raw[a][:].rearrange("p j (m t) -> p m j t", t=PACK)
-            nc.scalar.copy(dst[:, :SCALAR_SHARE], src[:, :SCALAR_SHARE])
-            nc.vector.tensor_copy(dst[:, SCALAR_SHARE:], src[:, SCALAR_SHARE:])
+            nc.scalar.copy(dst[:, :SCALAR_SHARE[a]], src[:, :SCALAR_SHARE[a]])
+            nc.vector.tensor_copy(dst[:, SCALAR_SHARE[a]:], src[:, SCALAR_SHARE[a]:])
             nc.vector.quantize_mx(out=gm_codes[a][:].bitcast(FP8X4), scales=gm_scales[a][:], in_=gm_bf[a][:])
 
         def predict(dst, a, t, entries):
@@ -143,8 +146,8 @@ def tile_list_villa_survey_step_kernel(
             first = CHUNK * (c % 2) + P * b
             return field_halves[c // 2, a][:, :, first : first + P]
 
-        def residual_on_vector(c, a):
-            for b in range(CHUNK // P):
+        def residual_on_vector(c, a, blocks=(0, 1)):
+            for b in blocks:
                 pred = pred_psum.tile([P, PACK, P], F32, name="pred")
                 for t in range(PACK):
                     predict(pred[:, t, :], a, t, slice(CHUNK * c + P * b, CHUNK * c + P * (b + 1)))
@@ -220,15 +223,18 @@ def tile_list_villa_survey_step_kernel(
                         start=(a == 0),
                         stop=(a == PASSES - 1),
                     )
-            scaled[piece] = sb("scaled%d_%d" % piece[:2], [P, width(piece)], F32)
-            nc.scalar.activation(scaled[piece][:], y[:], ACT.Copy, scale=steps[:, i : i + 1])
+            if piece == (0, 0, 0):
+                scaled[piece] = keep.tile([P, CHUNK], F32, name="first_scaled", tag="shared", align_bytes=64)[:]
+            else:
+                scaled[piece] = own("scaled", piece)
+            nc.scalar.activation(scaled[piece], y[:], ACT.Copy, scale=steps[:, i : i + 1])
 
         def own(kind, piece):
             return sb("%s%d_%d" % (kind, piece[0], piece[1]), [P, width(piece)], F32)[:]
 
         def gather_add(piece, dst):
             summed[piece] = dst
-            nc.vector.tensor_tensor(dst, window(piece), scaled[piece][:], ALU.add)
+            nc.vector.tensor_tensor(dst, window(piece), scaled[piece], ALU.add)
 
         def clamp(piece, dst):
             new[piece] = dst
@@ -253,13 +259,17 @@ def tile_list_villa_survey_step_kernel(
         residual_on_vector(0, 1)
         quantize_h(0)
         residual_on_vector(1, 1)
+        lead_back((0, 0, 0))
+        gather_add((0, 0, 0), own("summed", (0, 0, 0)))
+        h_scales[1] = keep.tile([P, PASSES * CHUNK], U8, name="h_scales1", tag="shared", align_bytes=64)
         quantize_h(1)
-
-        early = [(i, c, c) for c in range(2) for i in range(2)]
+        clamp((0, 0, 0), field_halves[0, 1][:, 0, CHUNK:])
+        scatter((0, 0, 0))
+        early = [(1, 0, 0), (0, 1, 1), (1, 1, 1)]
         for piece in early:
             lead_back(piece)
-        move((0, 0, 0))
-        move((1, 0, 0))
+        gather_add((1, 0, 0), new[0, 0, 0])
+        clamp((1, 0, 0), own("new", (1, 0, 0)))
         gather_add((0, 1, 1), own("summed", (0, 1, 1)))
         clamp((0, 1, 1), summed2[:, :CHUNK])
         gather_add((1, 1, 1), own("summed", (1, 1, 1)))

@@ -68,9 +68,9 @@ def tile_list_villa_survey_step_kernel(
         step_rows = sb("step_rows", [P, P], F32)
         summed2 = sb("summed2", [P, HALF], F32)
 
-        nc.gpsimd.memset(table_scales[:].bitcast(I32), 0)
+        nc.vector.memset(table_scales[:].bitcast(I32), 0)
+        nc.vector.memset(step_rows[:], 0.0)
         nc.vector.memset(b_scales[:].bitcast(I32), 0)
-        nc.gpsimd.memset(step_rows[:], 0.0)
         make_identity(nc, identity[:])
 
         def load_gm(a):
@@ -92,13 +92,13 @@ def tile_list_villa_survey_step_kernel(
 
         nc.sync.dma_start(offsets[:], offs)
         words = tab_words[0].rearrange("p t i -> p (t i)").bitcast(I32)
-        nc.sync.dma_start(table_words[:, :PASS], words[:, :PASS])
+        nc.sync.dma_start(table_words[:, : T // 2], words[:, : T // 2])
         for quad in range(QUADS):
             nc.sync.dma_start(
                 table_scales[32 * quad : 32 * quad + 4, :].bitcast(I32),
                 tab_scales[0, 4 * quad : 4 * quad + 4, :].bitcast(I32),
             )
-        nc.sync.dma_start(table_words[:, PASS:], words[:, PASS:])
+        nc.sync.dma_start(table_words[:, T // 2 :], words[:, T // 2 :])
         nc.sync.dma_start(step_rows[:TILES, :], step.rearrange("(i p) -> i p", p=P))
         step_turned = turn_psum.tile([P, P], F32, name="turn")
         nc.tensor.transpose(step_turned[:], step_rows[:], identity[:])

@@ -25,7 +25,8 @@ CHUNK = 256
 CHUNKS = S // CHUNK
 HALF = 2 * CHUNK
 QUADS = 4
-SCALAR_SHARE = (64, 36)
+SCALAR_SHARE = (84, 72)
+OVERLAP = 64
 
 
 def tile_list_villa_survey_step_kernel(
@@ -49,8 +50,8 @@ def tile_list_villa_survey_step_kernel(
         steps = sb("steps", [P, TILES], F32)
         maps = [sb("map%d" % i, [P, T], F32) for i in range(TILES)]
         gm_raw = [sb("gm_raw%d" % a, [P, PACK, PASS], F32) for a in range(PASSES)]
-        woven = sb("woven", [P, PASS * PACK], BF16)
-        gm_bf = [woven, woven]
+        woven = sb("woven", [P, 2 * PASS * PACK - OVERLAP], BF16)
+        gm_bf = [woven[:, PASS * PACK - OVERLAP :], woven[:, : PASS * PACK]]
         gm_codes = [sb("gm_codes%d" % a, [P, PASS], U32) for a in range(PASSES)]
         gm_scales = [sb("gm_scales%d" % a, [P, PASS], U8) for a in range(PASSES)]
         v_words = sb("v_words", [P, S], U32)
@@ -125,11 +126,11 @@ def tile_list_villa_survey_step_kernel(
         nc.vector.tensor_copy(v_words[:], table_words[:].bitcast(U32).indirect(offsets[:]))
 
         def quantize_gm(a):
-            dst = gm_bf[a][:].rearrange("p (t m j) -> p m j t", t=PACK, j=PACK)
+            dst = gm_bf[a].rearrange("p (t m j) -> p m j t", t=PACK, j=PACK)
             src = gm_raw[a][:].rearrange("p j (m t) -> p m j t", t=PACK)
             nc.scalar.copy(dst[:, :SCALAR_SHARE[a]], src[:, :SCALAR_SHARE[a]])
             nc.vector.tensor_copy(dst[:, SCALAR_SHARE[a]:], src[:, SCALAR_SHARE[a]:])
-            nc.vector.quantize_mx(out=gm_codes[a][:].bitcast(FP8X4), scales=gm_scales[a][:], in_=gm_bf[a][:])
+            nc.vector.quantize_mx(out=gm_codes[a][:].bitcast(FP8X4), scales=gm_scales[a][:], in_=gm_bf[a])
 
         def predict(dst, a, t, entries):
             nc.tensor.matmul_mx(
@@ -153,9 +154,9 @@ def tile_list_villa_survey_step_kernel(
                     predict(pred[:, t, :], a, t, slice(CHUNK * c + P * b, CHUNK * c + P * (b + 1)))
                 at = PACK * (CHUNK * a + P * b)
                 nc.vector.tensor_tensor(
-                    h_bf[c][:, at : at + PASS].rearrange("p (g i t) -> p g t i", i=2, t=PACK),
-                    measured(c, a, b).rearrange("p t (g i) -> p g t i", i=2),
-                    pred[:].rearrange("p t (g i) -> p g t i", i=2),
+                    h_bf[c][:, at : at + PASS].rearrange("p (g i t) -> p g t i", i=PACK, t=PACK),
+                    measured(c, a, b).rearrange("p t (g i) -> p g t i", i=PACK),
+                    pred[:].rearrange("p t (g i) -> p g t i", i=PACK),
                     ALU.subtract,
                 )
 

@@ -25,8 +25,11 @@ CHUNK = 256
 CHUNKS = S // CHUNK
 HALF = 2 * CHUNK
 QUADS = 4
+BANKS = 8
 SCALAR_SHARE = (84, 72)
 OVERLAP = 64
+SUM_BANK = {(2, 0): 0, (2, 1): 2, (3, 0): 6, (3, 1): 4}
+PAIR_BANK = {(2, 0): 0, (2, 1): 2, (3, 0): 6, (3, 1): 7}
 
 
 def tile_list_villa_survey_step_kernel(
@@ -35,18 +38,17 @@ def tile_list_villa_survey_step_kernel(
     nc = tc.nc
     with ExitStack() as ctx:
         keep = ctx.enter_context(tc.tile_pool(name="keep", bufs=1))
-        pred_psum = ctx.enter_context(tc.psum_pool(name="pred_psum", bufs=3))
-        turn_psum = ctx.enter_context(tc.psum_pool(name="turn_psum", bufs=3))
-        y_psum = ctx.enter_context(tc.psum_pool(name="y_psum", bufs=2))
+        psum = ctx.enter_context(tc.psum_pool(name="psum", bufs=1))
+        banks = [psum.tile([P, PASS], F32, name="bank%d" % n, tag="bank%d" % n) for n in range(BANKS)]
 
-        def sb(name, shape, dtype):
-            return keep.tile(shape, dtype, name=name, tag=name, align_bytes=64)
+        def sb(name, shape, dtype, slot=None):
+            return keep.tile(shape, dtype, name=name, tag=slot or name, align_bytes=64)
 
         offsets = keep.tile([P, S // 16], U16, name="offsets")
         table_scales = sb("table_scales", [P, T], U8)
         table_words = sb("table_words", [P, T], I32)
-        b_scales = sb("b_scales", [P, PASSES * K], U8)
-        b_words = [sb("b_words%d" % n, [P, PASSES * 2 * P], I32) for n in range(TILES // 2)]
+        b_scales = sb("b_scales", [P, K], U8)
+        b_words = [sb("b_words%d" % i, [P, PASSES * P], I32) for i in range(TILES)]
         steps = sb("steps", [P, TILES], F32)
         maps = [sb("map%d" % i, [P, T], F32) for i in range(TILES)]
         gm_raw = [sb("gm_raw%d" % a, [P, PACK, PASS], F32) for a in range(PASSES)]
@@ -59,15 +61,19 @@ def tile_list_villa_survey_step_kernel(
         identity = sb("identity", [P, P], F32)
         h_bf, h_codes, h_scales = [], [], []
         for c in range(CHUNKS):
-            h_bf.append(sb("h_bf%d" % c, [P, PASSES * CHUNK * PACK], BF16))
+            h_bf.append(h_bf[0] if c == 1 else sb("h_bf%d" % c, [P, PASSES * CHUNK * PACK], BF16))
             h_codes.append(sb("h_codes%d" % c, [P, PASSES * CHUNK], U32))
-            h_scales.append(None if c == 1 else sb("h_scales%d" % c, [P, PASSES * CHUNK], U8))
-        field_halves = {}
-        for half in range(S // HALF):
+            h_scales.append(None if c in (1, 2) else sb("h_scales%d" % c, [P, PASSES * CHUNK], U8))
+        field_first = sb("field_first", [P, PACK, HALF], F32)
+        field_second = [sb("field_second%d" % c, [P, PACK, CHUNK], F32) for c in range(2)]
+        field_late = [sb("field_late%d" % a, [P, PACK, HALF], F32) for a in range(PASSES)]
+        negated, rounded = {}, {}
+        for c in (2, 3):
+            negated[c] = sb("negated%d" % c, [P, PASSES * PACK * CHUNK], F32)
             for a in range(PASSES):
-                field_halves[half, a] = sb("field%d_%d" % (half, a), [P, PACK, HALF], F32)
+                rounded[c, a] = sb("rounded%d_%d" % (c, a), [P, PASS], F32)
+        tile2_scaled = sb("tile2_scaled", [P, HALF], F32)
         step_rows = sb("step_rows", [P, P], F32)
-        summed2 = sb("summed2", [P, HALF], F32)
 
         nc.vector.memset(table_scales[:].bitcast(I32), 0)
         nc.vector.memset(step_rows[:], 0.0)
@@ -78,14 +84,14 @@ def tile_list_villa_survey_step_kernel(
             columns = gm[:, PASS * a : PASS * (a + 1)]
             nc.sync.dma_start(gm_raw[a][:], columns.rearrange("(p j) c -> p j c", j=PACK))
 
-        def load_field(half, a):
-            rows = field[PASS * a : PASS * (a + 1), HALF * half : HALF * (half + 1)]
-            nc.sync.dma_start(field_halves[half, a][:], rows.rearrange("(p t) j -> p t j", t=PACK))
+        def load_field(dst, a, first, count=HALF):
+            rows = field[PASS * a : PASS * (a + 1), first : first + count]
+            nc.sync.dma_start(dst[:], rows.rearrange("(p t) j -> p t j", t=PACK))
 
-        def load_back_words(n):
+        def load_back_words(i):
             nc.sync.dma_start(
-                b_words[n][:].rearrange("p (a c) -> p a c", a=PASSES),
-                back_words.rearrange("a p c i -> p a (c i)").bitcast(I32)[:, :, 2 * P * n : 2 * P * (n + 1)],
+                b_words[i][:].rearrange("p (a c) -> p a c", a=PASSES),
+                back_words.rearrange("a p c i -> p a (c i)").bitcast(I32)[:, :, P * i : P * (i + 1)],
             )
 
         def load_map(i):
@@ -101,25 +107,27 @@ def tile_list_villa_survey_step_kernel(
             )
         nc.sync.dma_start(table_words[:, T // 2 :], words[:, T // 2 :])
         nc.sync.dma_start(step_rows[:TILES, :], step.rearrange("(i p) -> i p", p=P))
-        step_turned = turn_psum.tile([P, P], F32, name="turn")
-        nc.tensor.transpose(step_turned[:], step_rows[:], identity[:])
-        nc.scalar.copy(steps[:], step_turned[:, :TILES])
+        nc.tensor.transpose(banks[-1][:, :P], step_rows[:], identity[:])
+        nc.scalar.copy(steps[:], banks[-1][:, :TILES])
         load_gm(0)
-        load_gm(1)
-        load_field(0, 0)
-        load_field(0, 1)
         for quad in range(QUADS):
             nc.sync.dma_start(
-                b_scales[32 * quad : 32 * quad + 4, :].bitcast(I32).rearrange("r (a c) -> r a c", a=PASSES),
-                back_scales[:, 4 * quad : 4 * quad + 4, :].bitcast(I32).rearrange("a r c -> r a c"),
+                b_scales[32 * quad + 4 : 32 * quad + 12, :].bitcast(I32),
+                back_scales[:, 4 * quad : 4 * quad + 4, :].bitcast(I32),
             )
+        load_gm(1)
+        load_field(field_first, 0, 0)
+        load_field(field_second[0], 1, 0, CHUNK)
         load_back_words(0)
+        load_field(field_second[1], 1, CHUNK, CHUNK)
         load_map(0)
-        load_map(1)
-        load_field(1, 0)
         load_back_words(1)
+        load_map(1)
+        load_back_words(2)
+        load_back_words(3)
         load_map(2)
-        load_field(1, 1)
+        load_field(field_late[0], 0, HALF)
+        load_field(field_late[1], 1, HALF)
         load_map(3)
 
         nc.vector.tensor_copy(v_scales[:], table_scales[:].indirect(offsets[:]))
@@ -128,8 +136,8 @@ def tile_list_villa_survey_step_kernel(
         def quantize_gm(a):
             dst = gm_bf[a].rearrange("p (t m j) -> p m j t", t=PACK, j=PACK)
             src = gm_raw[a][:].rearrange("p j (m t) -> p m j t", t=PACK)
-            nc.scalar.copy(dst[:, :SCALAR_SHARE[a]], src[:, :SCALAR_SHARE[a]])
-            nc.vector.tensor_copy(dst[:, SCALAR_SHARE[a]:], src[:, SCALAR_SHARE[a]:])
+            nc.scalar.copy(dst[:, : SCALAR_SHARE[a]], src[:, : SCALAR_SHARE[a]])
+            nc.vector.tensor_copy(dst[:, SCALAR_SHARE[a] :], src[:, SCALAR_SHARE[a] :])
             nc.vector.quantize_mx(out=gm_codes[a][:].bitcast(FP8X4), scales=gm_scales[a][:], in_=gm_bf[a])
 
         def predict(dst, a, t, entries):
@@ -143,59 +151,63 @@ def tile_list_villa_survey_step_kernel(
                 stop=True,
             )
 
-        def measured(c, a, b):
-            first = CHUNK * (c % 2) + P * b
-            return field_halves[c // 2, a][:, :, first : first + P]
-
-        def residual_on_vector(c, a, blocks=(0, 1)):
-            for b in blocks:
-                pred = pred_psum.tile([P, PACK, P], F32, name="pred")
+        def residual_on_vector(c, a, first_bank):
+            for b in range(CHUNK // P):
+                pred = banks[first_bank + b][:].rearrange("p (t j) -> p t j", t=PACK)
+                first = CHUNK * c + P * b
                 for t in range(PACK):
-                    predict(pred[:, t, :], a, t, slice(CHUNK * c + P * b, CHUNK * c + P * (b + 1)))
+                    predict(pred[:, t, :], a, t, slice(first, first + P))
                 at = PACK * (CHUNK * a + P * b)
+                measured = field_second[c][:, :, P * b : P * (b + 1)] if a else field_first[:, :, first : first + P]
                 nc.vector.tensor_tensor(
                     h_bf[c][:, at : at + PASS].rearrange("p (g i t) -> p g t i", i=PACK, t=PACK),
-                    measured(c, a, b).rearrange("p t (g i) -> p g t i", i=PACK),
-                    pred[:].rearrange("p t (g i) -> p g t i", i=PACK),
+                    measured.rearrange("p t (g i) -> p g t i", i=PACK),
+                    pred.rearrange("p t (g i) -> p g t i", i=PACK),
                     ALU.subtract,
                 )
 
-        def negate_predictions(a, first_chunk):
-            first = CHUNK * first_chunk
-            for t in range(PACK):
-                pred = turn_psum.tile([P, S - first], F32, name="turn")
-                predict(pred[:], a, t, slice(first, S))
-                nc.scalar.activation(field_halves[0, a][:, t, first - HALF :], pred[:], ACT.Copy, scale=-1.0)
+        def negate_predictions(c, a, first_bank):
+            for u in range(2):
+                bank = banks[first_bank + u]
+                for e in range(2):
+                    predict(bank[:, CHUNK * e : CHUNK * (e + 1)], a, 2 * u + e, slice(CHUNK * c, CHUNK * (c + 1)))
+                at = PASS * (2 * a + u)
+                nc.scalar.activation(negated[c][:, at : at + PASS], bank[:], ACT.Copy, scale=-1.0)
 
-        def residual_by_transposes(c, a):
-            negated = field_halves[0, a]
-            rounded = sb("rounded%d_%d" % (c, a), [P, PASS], F32)
+        def turn_predictions(c, a):
             for b in range(CHUNK // P):
+                bank = banks[SUM_BANK[c, a] + b]
+                for t in range(PACK):
+                    at = CHUNK * (PACK * a + t) + P * b
+                    nc.tensor.matmul(
+                        bank[:, P * t : P * (t + 1)], negated[c][:, at : at + P], identity[:],
+                        start=(t == 0), stop=False, is_transpose=True,
+                    )
+
+        def finish_residual(c, a):
+            for b in range(CHUNK // P):
+                bank = banks[SUM_BANK[c, a] + b]
                 first = CHUNK * (c % 2) + P * b
-                turned = turn_psum.tile([P, PACK, P], F32, name="turn")
                 for t in range(PACK):
                     nc.tensor.matmul(
-                        turned[:, t, :], measured(c, a, b)[:, t, :], identity[:],
-                        start=True, stop=False, is_transpose=True,
+                        bank[:, P * t : P * (t + 1)], field_late[a][:, t, first : first + P], identity[:],
+                        start=False, stop=(t == PACK - 1), is_transpose=True,
                     )
-                    nc.tensor.matmul(
-                        turned[:, t, :], negated[:, t, first : first + P], identity[:],
-                        start=False, stop=True, is_transpose=True,
-                    )
+                block = rounded[c, a][:, 2 * P * b : 2 * P * (b + 1)]
                 nc.scalar.activation(
-                    rounded[:, 2 * P * b : 2 * P * (b + 1)].bitcast(BF16).rearrange("j (u p e) -> j u p e", u=2, e=2),
-                    turned[:].rearrange("j (u e) p -> j u p e", u=2),
+                    block.bitcast(BF16).rearrange("j (u p e) -> j u p e", u=2, e=2),
+                    bank[:].rearrange("j (u e p) -> j u p e", u=2, e=2),
                     ACT.Copy,
                 )
-            pairs = turn_psum.tile([P, 2, 2, P], F32, name="turn")
-            for b in range(CHUNK // P):
-                for u in range(2):
-                    nc.tensor.transpose(pairs[:, b, u, :], rounded[:, P * (2 * b + u) : P * (2 * b + u + 1)], identity[:])
+
+        def turn_back(c, a):
+            pairs = banks[PAIR_BANK[c, a]]
+            for n in range(PACK):
+                nc.tensor.transpose(pairs[:, P * n : P * (n + 1)], rounded[c, a][:, P * n : P * (n + 1)], identity[:])
             nc.scalar.copy(
                 h_bf[c][:].bitcast(F32)[:, PASS * a : PASS * (a + 1)].rearrange("p (b j u) -> p b j u", b=2, u=2),
-                pairs[:].rearrange("p b u j -> p b j u"),
+                pairs[:].rearrange("p (b u j) -> p b j u", b=2, u=2),
             )
-            return rounded
 
         def quantize_h(c):
             nc.vector.quantize_mx(out=h_codes[c][:].bitcast(FP8X4), scales=h_scales[c][:], in_=h_bf[c][:])
@@ -209,29 +221,25 @@ def tile_list_villa_survey_step_kernel(
             i, first, last = piece
             return maps[i][:].indirect(offsets[:, CHUNK * first // 16 : CHUNK * (last + 1) // 16])
 
-        def lead_back(piece):
+        def own(kind, piece, slot=None):
+            return sb("%s%d_%d" % (kind, piece[0], piece[1]), [P, width(piece)], F32, slot)[:]
+
+        def lead_back(piece, bank, dst):
             i, first, last = piece
-            y = y_psum.tile([P, width(piece)], F32, name="y")
+            y = banks[bank][:, : width(piece)]
             for c in range(last, first - 1, -1):
                 for a in range(PASSES):
-                    word = 2 * P * a + P * (i % 2)
                     nc.tensor.matmul_mx(
                         out=y[:, CHUNK * (c - first) : CHUNK * (c - first + 1)],
-                        lhsT=b_words[i // 2][:, word : word + P].bitcast(FP8X4),
-                        lhsT_scale=b_scales[:, K * a + P * i : K * a + P * (i + 1)],
+                        lhsT=b_words[i][:, P * a : P * (a + 1)].bitcast(FP8X4),
+                        lhsT_scale=b_scales[4 * (a + 1) :, P * i : P * (i + 1)],
                         rhs=h_codes[c][:, CHUNK * a : CHUNK * (a + 1)].bitcast(FP8X4),
                         rhs_scale=h_scales[c][:, CHUNK * a : CHUNK * (a + 1)],
                         start=(a == 0),
                         stop=(a == PASSES - 1),
                     )
-            if piece == (0, 0, 0):
-                scaled[piece] = keep.tile([P, CHUNK], F32, name="first_scaled", tag="shared", align_bytes=64)[:]
-            else:
-                scaled[piece] = own("scaled", piece)
-            nc.scalar.activation(scaled[piece], y[:], ACT.Copy, scale=steps[:, i : i + 1])
-
-        def own(kind, piece):
-            return sb("%s%d_%d" % (kind, piece[0], piece[1]), [P, width(piece)], F32)[:]
+            scaled[piece] = dst
+            nc.scalar.activation(dst, y, ACT.Copy, scale=steps[:, i : i + 1])
 
         def gather_add(piece, dst):
             summed[piece] = dst
@@ -241,9 +249,9 @@ def tile_list_villa_survey_step_kernel(
             new[piece] = dst
             nc.scalar.activation(dst, summed[piece], ACT.Relu)
 
-        def move(piece):
-            gather_add(piece, own("summed", piece))
-            clamp(piece, own("new", piece))
+        def gather_chunk(i, c):
+            scaled[i, c, c] = scaled[i, 0, 1][:, CHUNK * c : CHUNK * (c + 1)]
+            gather_add((i, c, c), own("summed", (i, c, c)))
 
         def scatter(piece):
             i, first, last = piece
@@ -251,63 +259,79 @@ def tile_list_villa_survey_step_kernel(
             if last == CHUNKS - 1:
                 nc.sync.dma_start(out[P * i : P * (i + 1), :], maps[i][:])
 
-        h2_words = h_bf[2][:].bitcast(F32)
-
         for a in range(PASSES):
             quantize_gm(a)
-        residual_on_vector(0, 0)
-        residual_on_vector(1, 0)
-        residual_on_vector(0, 1)
+        residual_on_vector(0, 0, 0)
+        residual_on_vector(0, 1, 4)
         quantize_h(0)
-        residual_on_vector(1, 1)
-        lead_back((0, 0, 0))
-        gather_add((0, 0, 0), own("summed", (0, 0, 0)))
-        h_scales[1] = keep.tile([P, PASSES * CHUNK], U8, name="h_scales1", tag="shared", align_bytes=64)
+        residual_on_vector(1, 0, 2)
+        residual_on_vector(1, 1, 6)
+        negate_predictions(2, 0, 0)
+        negate_predictions(2, 1, 4)
+
+        lead_back((0, 0, 0), 4, own("scaled", (0, 0, 0), "first_slot"))
+        gather_add((0, 0, 0), negated[3][:, PASS - P : PASS + P])
+        h_scales[1] = sb("h_scales1", [P, PASSES * CHUNK], U8, "first_slot")
         quantize_h(1)
-        clamp((0, 0, 0), field_halves[0, 1][:, 0, CHUNK:])
+        clamp((0, 0, 0), field_second[1][:, 0, :])
         scatter((0, 0, 0))
-        early = [(1, 0, 0), (0, 1, 1), (1, 1, 1)]
-        for piece in early:
-            lead_back(piece)
+
+        held = [(0, 1, 1), (1, 1, 1)]
+        lead_back((1, 0, 0), 1, tile2_scaled[:, :CHUNK])
+        for n, piece in enumerate(held):
+            lead_back(piece, 2 + n, own("scaled", piece))
         gather_add((1, 0, 0), new[0, 0, 0])
         clamp((1, 0, 0), own("new", (1, 0, 0)))
-        gather_add((0, 1, 1), own("summed", (0, 1, 1)))
-        clamp((0, 1, 1), summed2[:, :CHUNK])
-        gather_add((1, 1, 1), own("summed", (1, 1, 1)))
-        clamp((1, 1, 1), h2_words[:, PASS + P : PASS + P + CHUNK])
-        for piece in early:
+        for piece in held:
+            gather_add(piece, own("summed", piece))
+        scatter((1, 0, 0))
+
+        negate_predictions(3, 0, 4)
+        lead_back((2, 0, 1), 4, tile2_scaled[:])
+        lead_back((3, 0, 1), 5, own("scaled", (3, 0, 1), "second_slot"))
+        negate_predictions(3, 1, 4)
+
+        for c, piece in enumerate(held):
+            gather_chunk(2, c)
+            clamp(piece, scaled[2, c, c])
+        new[2, 0, 1] = own("new", (2, 0, 1))
+        for c in range(2):
+            clamp((2, c, c), new[2, 0, 1][:, CHUNK * c : CHUNK * (c + 1)])
+        for piece in held + [(2, 0, 1)]:
             scatter(piece)
 
-        negate_predictions(0, 2)
-        residual_by_transposes(2, 0)
-        lead_back((2, 0, 1))
-        lead_back((3, 0, 1))
-        negate_predictions(1, 3)
-        gather_add((2, 0, 1), summed2[:])
-        residual_on_vector(2, 1)
+        units = [(c, a) for c in (2, 3) for a in range(PASSES)]
+        for c, a in units:
+            turn_predictions(c, a)
+        for c, a in units:
+            finish_residual(c, a)
+            turn_back(c, a)
+
+        for c in range(2):
+            gather_chunk(3, c)
+        h_scales[2] = sb("h_scales2", [P, PASSES * CHUNK], U8, "second_slot")
         quantize_h(2)
-        clamp((2, 0, 1), h2_words[:, :PASS])
-        gather_add((3, 0, 1), h2_words[:, PASS:])
-        clamp((3, 0, 1), summed2[:])
-        scatter((2, 0, 1))
+        new[3, 0, 1] = rounded[2, 1][:]
+        for c in range(2):
+            clamp((3, c, c), new[3, 0, 1][:, CHUNK * c : CHUNK * (c + 1)])
         scatter((3, 0, 1))
 
-        residual_by_transposes(3, 0)
-        last_rounded = residual_by_transposes(3, 1)
+        middle = [(0, 2, 2), (1, 2, 2)]
+        for n, piece in enumerate(middle):
+            lead_back(piece, SUM_BANK[3, 1] + n, own("scaled", piece))
+        for piece in middle:
+            gather_add(piece, own("summed", piece))
+        clamp((0, 2, 2), own("new", (0, 2, 2)))
         quantize_h(3)
-        lead_back((0, 2, 2))
-        lead_back((1, 2, 2))
-        gather_add((0, 2, 2), own("summed", (0, 2, 2)))
-        clamp((0, 2, 2), last_rounded[:, CHUNK:])
-        gather_add((1, 2, 2), own("summed", (1, 2, 2)))
-        clamp((1, 2, 2), summed[0, 2, 2])
-        scatter((0, 2, 2))
-        scatter((1, 2, 2))
+        clamp((1, 2, 2), h_bf[3][:].bitcast(F32)[:, :CHUNK])
+        for piece in middle:
+            scatter(piece)
 
         late = [(0, 3, 3), (1, 3, 3), (2, 2, 3), (3, 2, 3)]
+        for bank, piece in enumerate(late):
+            lead_back(piece, bank, own("scaled", piece))
         for piece in late:
-            lead_back(piece)
-        for piece in late:
-            move(piece)
+            gather_add(piece, own("summed", piece))
+            clamp(piece, own("new", piece))
         for piece in late:
             scatter(piece)

@@ -26,7 +26,7 @@ CHUNKS = S // CHUNK
 HALF = 2 * CHUNK
 QUADS = 4
 BANKS = 8
-SCALAR_SHARE = (84, 72)
+SCALAR_SHARE = (84, 48)
 OVERLAP = 64
 SUM_BANK = {(2, 0): 0, (2, 1): 2, (3, 0): 6, (3, 1): 4}
 PAIR_BANK = {(2, 0): 0, (2, 1): 2, (3, 0): 6, (3, 1): 7}
@@ -64,8 +64,10 @@ def tile_list_villa_survey_step_kernel(
             h_bf.append(h_bf[0] if c == 1 else sb("h_bf%d" % c, [P, PASSES * CHUNK * PACK], BF16))
             h_codes.append(sb("h_codes%d" % c, [P, PASSES * CHUNK], U32))
             h_scales.append(None if c in (1, 2) else sb("h_scales%d" % c, [P, PASSES * CHUNK], U8))
-        field_first = sb("field_first", [P, PACK, HALF], F32)
-        field_second = [sb("field_second%d" % c, [P, PACK, CHUNK], F32) for c in range(2)]
+        field_early = {}
+        for c in range(2):
+            for a in range(PASSES):
+                field_early[c, a] = sb("field_early%d_%d" % (c, a), [P, PACK, CHUNK], F32)
         field_late = [sb("field_late%d" % a, [P, PACK, HALF], F32) for a in range(PASSES)]
         negated, rounded = {}, {}
         for c in (2, 3):
@@ -84,7 +86,7 @@ def tile_list_villa_survey_step_kernel(
             columns = gm[:, PASS * a : PASS * (a + 1)]
             nc.sync.dma_start(gm_raw[a][:], columns.rearrange("(p j) c -> p j c", j=PACK))
 
-        def load_field(dst, a, first, count=HALF):
+        def load_field(dst, a, first, count):
             rows = field[PASS * a : PASS * (a + 1), first : first + count]
             nc.sync.dma_start(dst[:], rows.rearrange("(p t) j -> p t j", t=PACK))
 
@@ -116,18 +118,19 @@ def tile_list_villa_survey_step_kernel(
                 back_scales[:, 4 * quad : 4 * quad + 4, :].bitcast(I32),
             )
         load_gm(1)
-        load_field(field_first, 0, 0)
-        load_field(field_second[0], 1, 0, CHUNK)
+        for a in range(PASSES):
+            load_field(field_early[0, a], a, 0, CHUNK)
         load_back_words(0)
-        load_field(field_second[1], 1, CHUNK, CHUNK)
+        for a in range(PASSES):
+            load_field(field_early[1, a], a, CHUNK, CHUNK)
         load_map(0)
         load_back_words(1)
         load_map(1)
         load_back_words(2)
         load_back_words(3)
         load_map(2)
-        load_field(field_late[0], 0, HALF)
-        load_field(field_late[1], 1, HALF)
+        for a in range(PASSES):
+            load_field(field_late[a], a, HALF, HALF)
         load_map(3)
 
         nc.vector.tensor_copy(v_scales[:], table_scales[:].indirect(offsets[:]))
@@ -158,7 +161,7 @@ def tile_list_villa_survey_step_kernel(
                 for t in range(PACK):
                     predict(pred[:, t, :], a, t, slice(first, first + P))
                 at = PACK * (CHUNK * a + P * b)
-                measured = field_second[c][:, :, P * b : P * (b + 1)] if a else field_first[:, :, first : first + P]
+                measured = field_early[c, a][:, :, P * b : P * (b + 1)]
                 nc.vector.tensor_tensor(
                     h_bf[c][:, at : at + PASS].rearrange("p (g i t) -> p g t i", i=PACK, t=PACK),
                     measured.rearrange("p t (g i) -> p g t i", i=PACK),
@@ -273,7 +276,7 @@ def tile_list_villa_survey_step_kernel(
         gather_add((0, 0, 0), negated[3][:, PASS - P : PASS + P])
         h_scales[1] = sb("h_scales1", [P, PASSES * CHUNK], U8, "first_slot")
         quantize_h(1)
-        clamp((0, 0, 0), field_second[1][:, 0, :])
+        clamp((0, 0, 0), field_early[1, 1][:, 0, :])
         scatter((0, 0, 0))
 
         held = [(0, 1, 1), (1, 1, 1)]

@@ -61,9 +61,12 @@ def tile_list_villa_survey_step_kernel(
         identity = sb("identity", [P, P], F32)
         h_bf, h_codes, h_scales = [], [], []
         for c in range(CHUNKS):
-            h_bf.append(h_bf[0] if c == 1 else sb("h_bf%d" % c, [P, PASSES * CHUNK * PACK], BF16))
+            if c < 2:
+                h_bf.append(h_bf[0] if c == 1 else sb("h_bf0", [P, PASSES * CHUNK * PACK], BF16))
             h_codes.append(sb("h_codes%d" % c, [P, PASSES * CHUNK], U32))
             h_scales.append(None if c in (1, 2) else sb("h_scales%d" % c, [P, PASSES * CHUNK], U8))
+        h_late = sb("h_late", [P, 3 * CHUNK * PACK], BF16)
+        h_bf.extend([h_late[:, CHUNK * PACK :], h_late[:, : 2 * CHUNK * PACK]])
         field_early = {}
         for c in range(2):
             for a in range(PASSES):
@@ -73,7 +76,8 @@ def tile_list_villa_survey_step_kernel(
         for c in (2, 3):
             negated[c] = sb("negated%d" % c, [P, PASSES * PACK * CHUNK], F32)
             for a in range(PASSES):
-                rounded[c, a] = sb("rounded%d_%d" % (c, a), [P, PASS], F32)
+                if c == 2:
+                    rounded[c, a] = sb("rounded%d_%d" % (c, a), [P, PASS], F32)
         tile2_scaled = sb("tile2_scaled", [P, HALF], F32)
         step_rows = sb("step_rows", [P, P], F32)
 
@@ -252,9 +256,18 @@ def tile_list_villa_survey_step_kernel(
             new[piece] = dst
             nc.scalar.activation(dst, summed[piece], ACT.Relu)
 
+        def residual_on_gpsimd(a):
+            at = CHUNK * PACK * a
+            nc.gpsimd.tensor_tensor(
+                h_bf[3][:, at : at + CHUNK * PACK].rearrange("p (g i t) -> p g t i", i=PACK, t=PACK),
+                field_late[a][:, :, CHUNK:].rearrange("p t (g i) -> p g t i", i=PACK),
+                negated[3][:, at : at + CHUNK * PACK].rearrange("p (t g i) -> p g t i", t=PACK, i=PACK),
+                ALU.add,
+            )
+
         def gather_chunk(i, c):
             scaled[i, c, c] = scaled[i, 0, 1][:, CHUNK * c : CHUNK * (c + 1)]
-            gather_add((i, c, c), own("summed", (i, c, c)))
+            gather_add((i, c, c), h_bf[3].bitcast(F32)[:, :CHUNK] if (i, c) == (2, 1) else own("summed", (i, c, c)))
 
         def scatter(piece):
             i, first, last = piece
@@ -303,7 +316,8 @@ def tile_list_villa_survey_step_kernel(
         for piece in held + [(2, 0, 1)]:
             scatter(piece)
 
-        units = [(c, a) for c in (2, 3) for a in range(PASSES)]
+        residual_on_gpsimd(0)
+        units = [(2, a) for a in range(PASSES)]
         for c, a in units:
             turn_predictions(c, a)
         for c, a in units:
@@ -314,6 +328,7 @@ def tile_list_villa_survey_step_kernel(
             gather_chunk(3, c)
         h_scales[2] = sb("h_scales2", [P, PASSES * CHUNK], U8, "second_slot")
         quantize_h(2)
+        residual_on_gpsimd(1)
         new[3, 0, 1] = rounded[2, 1][:]
         for c in range(2):
             clamp((3, c, c), new[3, 0, 1][:, CHUNK * c : CHUNK * (c + 1)])

@@ -21,15 +21,12 @@ PACK = 4
 PASS = P * PACK
 PASSES = H // PASS
 TILES = K // P
-CHUNK = 256
-CHUNKS = S // CHUNK
-HALF = 2 * CHUNK
 QUADS = 4
 BANKS = 8
-SCALAR_SHARE = (84, 48)
+A, B, C, D = range(4)
+EDGES = (0, 256, 384, 640, 1024)
+WIDE = 2 * P
 OVERLAP = 64
-SUM_BANK = {(2, 0): 0, (2, 1): 2, (3, 0): 6, (3, 1): 4}
-PAIR_BANK = {(2, 0): 0, (2, 1): 2, (3, 0): 6, (3, 1): 7}
 
 
 def tile_list_villa_survey_step_kernel(
@@ -44,6 +41,9 @@ def tile_list_villa_survey_step_kernel(
         def sb(name, shape, dtype, slot=None):
             return keep.tile(shape, dtype, name=name, tag=slot or name, align_bytes=64)
 
+        def size(c):
+            return EDGES[c + 1] - EDGES[c]
+
         offsets = keep.tile([P, S // 16], U16, name="offsets")
         table_scales = sb("table_scales", [P, T], U8)
         table_words = sb("table_words", [P, T], I32)
@@ -51,7 +51,7 @@ def tile_list_villa_survey_step_kernel(
         b_words = [sb("b_words%d" % i, [P, PASSES * P], I32) for i in range(TILES)]
         steps = sb("steps", [P, TILES], F32)
         maps = [sb("map%d" % i, [P, T], F32) for i in range(TILES)]
-        gm_raw = [sb("gm_raw%d" % a, [P, PACK, PASS], F32) for a in range(PASSES)]
+        gm_raw = [[sb("gm_raw%d_%d" % (a, n), [P, PACK, WIDE], F32) for n in range(2)] for a in range(PASSES)]
         woven = sb("woven", [P, 2 * PASS * PACK - OVERLAP], BF16)
         gm_bf = [woven[:, PASS * PACK - OVERLAP :], woven[:, : PASS * PACK]]
         gm_codes = [sb("gm_codes%d" % a, [P, PASS], U32) for a in range(PASSES)]
@@ -59,27 +59,25 @@ def tile_list_villa_survey_step_kernel(
         v_words = sb("v_words", [P, S], U32)
         v_scales = sb("v_scales", [P, S], U8)
         identity = sb("identity", [P, P], F32)
-        h_bf, h_codes, h_scales = [], [], []
-        for c in range(CHUNKS):
-            if c < 2:
-                h_bf.append(h_bf[0] if c == 1 else sb("h_bf0", [P, PASSES * CHUNK * PACK], BF16))
-            h_codes.append(sb("h_codes%d" % c, [P, PASSES * CHUNK], U32))
-            h_scales.append(None if c in (1, 2) else sb("h_scales%d" % c, [P, PASSES * CHUNK], U8))
-        h_late = sb("h_late", [P, 3 * CHUNK * PACK], BF16)
-        h_bf.extend([h_late[:, CHUNK * PACK :], h_late[:, : 2 * CHUNK * PACK]])
-        field_early = {}
-        for c in range(2):
-            for a in range(PASSES):
-                field_early[c, a] = sb("field_early%d_%d" % (c, a), [P, PACK, CHUNK], F32)
-        field_late = [sb("field_late%d" % a, [P, PACK, HALF], F32) for a in range(PASSES)]
-        negated, rounded = {}, {}
-        for c in (2, 3):
-            negated[c] = sb("negated%d" % c, [P, PASSES * PACK * CHUNK], F32)
-            for a in range(PASSES):
-                if c == 2:
-                    rounded[c, a] = sb("rounded%d_%d" % (c, a), [P, PASS], F32)
-        tile2_scaled = sb("tile2_scaled", [P, HALF], F32)
         step_rows = sb("step_rows", [P, P], F32)
+        h_bf, h_codes, h_scales = {}, {}, {}
+        for c in (A, B, C, D):
+            h_codes[c] = sb("h_codes%d" % c, [P, PASSES * size(c)], U32)
+        h_scales[A] = sb("h_scales0", [P, PASSES * size(A)], U8)
+        h_bf[A] = sb("h_early", [P, PASSES * PACK * size(A)], BF16)[:]
+        h_bf[B] = h_bf[A][:, : PASSES * PACK * size(B)]
+        h_late = sb("h_late", [P, PASSES * PACK * (size(C) + size(D)) - PASS], BF16)
+        h_bf[C] = h_late[:, : PASSES * PACK * size(C)]
+        h_bf[D] = h_late[:, PASSES * PACK * size(C) - PASS :]
+        measured, negated = {}, {}
+        for c in (A, B, C, D):
+            for a in range(PASSES):
+                measured[c, a] = sb("field%d_%d" % (c, a), [P, PACK, size(c)], F32)
+        for c in (C, D):
+            for a in range(PASSES):
+                negated[c, a] = sb("negated%d_%d" % (c, a), [P, PACK * size(c)], F32)[:]
+        rounded_d = sb("rounded_d", [P, 3 * WIDE], F32)
+        rounded_c = sb("rounded_c", [P, PASS], F32)
 
         nc.vector.memset(table_scales[:].bitcast(I32), 0)
         nc.vector.memset(step_rows[:], 0.0)
@@ -87,12 +85,13 @@ def tile_list_villa_survey_step_kernel(
         make_identity(nc, identity[:])
 
         def load_gm(a):
-            columns = gm[:, PASS * a : PASS * (a + 1)]
-            nc.sync.dma_start(gm_raw[a][:], columns.rearrange("(p j) c -> p j c", j=PACK))
+            for n in range(2):
+                columns = gm[:, PASS * a + WIDE * n : PASS * a + WIDE * (n + 1)]
+                nc.sync.dma_start(gm_raw[a][n][:], columns.rearrange("(p j) c -> p j c", j=PACK))
 
-        def load_field(dst, a, first, count):
-            rows = field[PASS * a : PASS * (a + 1), first : first + count]
-            nc.sync.dma_start(dst[:], rows.rearrange("(p t) j -> p t j", t=PACK))
+        def load_field(c, a):
+            rows = field[PASS * a : PASS * (a + 1), EDGES[c] : EDGES[c + 1]]
+            nc.sync.dma_start(measured[c, a][:], rows.rearrange("(p t) j -> p t j", t=PACK))
 
         def load_back_words(i):
             nc.sync.dma_start(
@@ -122,234 +121,266 @@ def tile_list_villa_survey_step_kernel(
                 back_scales[:, 4 * quad : 4 * quad + 4, :].bitcast(I32),
             )
         load_gm(1)
-        for a in range(PASSES):
-            load_field(field_early[0, a], a, 0, CHUNK)
+        load_field(A, 0)
+        load_field(A, 1)
         load_back_words(0)
-        for a in range(PASSES):
-            load_field(field_early[1, a], a, CHUNK, CHUNK)
+        load_field(B, 0)
+        load_field(B, 1)
         load_map(0)
         load_back_words(1)
         load_map(1)
         load_back_words(2)
+        load_field(C, 0)
         load_back_words(3)
         load_map(2)
-        for a in range(PASSES):
-            load_field(field_late[a], a, HALF, HALF)
+        load_field(C, 1)
         load_map(3)
+        load_field(D, 0)
+        load_field(D, 1)
 
         nc.vector.tensor_copy(v_scales[:], table_scales[:].indirect(offsets[:]))
         nc.vector.tensor_copy(v_words[:], table_words[:].bitcast(U32).indirect(offsets[:]))
 
         def quantize_gm(a):
             dst = gm_bf[a].rearrange("p (t m j) -> p m j t", t=PACK, j=PACK)
-            src = gm_raw[a][:].rearrange("p j (m t) -> p m j t", t=PACK)
-            nc.scalar.copy(dst[:, : SCALAR_SHARE[a]], src[:, : SCALAR_SHARE[a]])
-            nc.vector.tensor_copy(dst[:, SCALAR_SHARE[a] :], src[:, SCALAR_SHARE[a] :])
+            for n in range(2):
+                weave = nc.vector.tensor_copy if (a, n) == (PASSES - 1, 1) else nc.scalar.copy
+                src = gm_raw[a][n][:].rearrange("p j (m t) -> p m j t", t=PACK)
+                weave(dst[:, P // 2 * n : P // 2 * (n + 1)], src)
             nc.vector.quantize_mx(out=gm_codes[a][:].bitcast(FP8X4), scales=gm_scales[a][:], in_=gm_bf[a])
 
-        def predict(dst, a, t, entries):
+        def predict(dst, a, t, first, count):
             nc.tensor.matmul_mx(
                 out=dst,
                 lhsT=gm_codes[a][:, P * t : P * (t + 1)].bitcast(FP8X4),
                 lhsT_scale=gm_scales[a][:, P * t : P * (t + 1)],
-                rhs=v_words[:, entries].bitcast(FP8X4),
-                rhs_scale=v_scales[:, entries],
+                rhs=v_words[:, first : first + count].bitcast(FP8X4),
+                rhs_scale=v_scales[:, first : first + count],
                 start=True,
                 stop=True,
             )
 
         def residual_on_vector(c, a, first_bank):
-            for b in range(CHUNK // P):
+            for b in range(size(c) // P):
                 pred = banks[first_bank + b][:].rearrange("p (t j) -> p t j", t=PACK)
-                first = CHUNK * c + P * b
                 for t in range(PACK):
-                    predict(pred[:, t, :], a, t, slice(first, first + P))
-                at = PACK * (CHUNK * a + P * b)
-                measured = field_early[c, a][:, :, P * b : P * (b + 1)]
+                    predict(pred[:, t, :], a, t, EDGES[c] + P * b, P)
+                at = PACK * (size(c) * a + P * b)
                 nc.vector.tensor_tensor(
                     h_bf[c][:, at : at + PASS].rearrange("p (g i t) -> p g t i", i=PACK, t=PACK),
-                    measured.rearrange("p t (g i) -> p g t i", i=PACK),
+                    measured[c, a][:, :, P * b : P * (b + 1)].rearrange("p t (g i) -> p g t i", i=PACK),
                     pred.rearrange("p t (g i) -> p g t i", i=PACK),
                     ALU.subtract,
                 )
 
-        def negate_predictions(c, a, first_bank):
+        def negate_wide(a, two_banks):
             for u in range(2):
-                bank = banks[first_bank + u]
+                bank = banks[two_banks[u]]
                 for e in range(2):
-                    predict(bank[:, CHUNK * e : CHUNK * (e + 1)], a, 2 * u + e, slice(CHUNK * c, CHUNK * (c + 1)))
-                at = PASS * (2 * a + u)
-                nc.scalar.activation(negated[c][:, at : at + PASS], bank[:], ACT.Copy, scale=-1.0)
+                    predict(bank[:, WIDE * e : WIDE * (e + 1)], a, 2 * u + e, EDGES[C], WIDE)
+                nc.scalar.activation(negated[C, a][:, PASS * u : PASS * (u + 1)], bank[:], ACT.Copy, scale=-1.0)
 
-        def turn_predictions(c, a):
-            for b in range(CHUNK // P):
-                bank = banks[SUM_BANK[c, a] + b]
-                for t in range(PACK):
-                    at = CHUNK * (PACK * a + t) + P * b
-                    nc.tensor.matmul(
-                        bank[:, P * t : P * (t + 1)], negated[c][:, at : at + P], identity[:],
-                        start=(t == 0), stop=False, is_transpose=True,
-                    )
+        def negate(sheet, bank):
+            c, a, b = sheet
+            pred = banks[bank][:].rearrange("p (t j) -> p t j", t=PACK)
+            for t in range(PACK):
+                predict(pred[:, t, :], a, t, EDGES[c] + P * b, P)
+            dst = negated[c, a].rearrange("p (t j) -> p t j", t=PACK)[:, :, P * b : P * (b + 1)]
+            nc.scalar.activation(dst, pred, ACT.Copy, scale=-1.0)
 
-        def finish_residual(c, a):
-            for b in range(CHUNK // P):
-                bank = banks[SUM_BANK[c, a] + b]
-                first = CHUNK * (c % 2) + P * b
-                for t in range(PACK):
-                    nc.tensor.matmul(
-                        bank[:, P * t : P * (t + 1)], field_late[a][:, t, first : first + P], identity[:],
-                        start=False, stop=(t == PACK - 1), is_transpose=True,
-                    )
-                block = rounded[c, a][:, 2 * P * b : 2 * P * (b + 1)]
-                nc.scalar.activation(
-                    block.bitcast(BF16).rearrange("j (u p e) -> j u p e", u=2, e=2),
-                    bank[:].rearrange("j (u e p) -> j u p e", u=2, e=2),
-                    ACT.Copy,
+        def turn_negated(sheet, bank):
+            c, a, b = sheet
+            for t in range(PACK):
+                at = size(c) * t + P * b
+                nc.tensor.matmul(
+                    banks[bank][:, P * t : P * (t + 1)], negated[c, a][:, at : at + P], identity[:],
+                    start=(t == 0), stop=False, is_transpose=True,
                 )
 
-        def turn_back(c, a):
-            pairs = banks[PAIR_BANK[c, a]]
-            for n in range(PACK):
-                nc.tensor.transpose(pairs[:, P * n : P * (n + 1)], rounded[c, a][:, P * n : P * (n + 1)], identity[:])
-            nc.scalar.copy(
-                h_bf[c][:].bitcast(F32)[:, PASS * a : PASS * (a + 1)].rearrange("p (b j u) -> p b j u", b=2, u=2),
-                pairs[:].rearrange("p (b u j) -> p b j u", b=2, u=2),
+        def add_field(sheet, bank, dst):
+            c, a, b = sheet
+            for t in range(PACK):
+                nc.tensor.matmul(
+                    banks[bank][:, P * t : P * (t + 1)], measured[c, a][:, t, P * b : P * (b + 1)], identity[:],
+                    start=False, stop=(t == PACK - 1), is_transpose=True,
+                )
+            nc.scalar.activation(
+                dst.bitcast(BF16).rearrange("j (u p e) -> j u p e", u=2, e=2),
+                banks[bank][:].rearrange("j (u e p) -> j u p e", u=2, e=2),
+                ACT.Copy,
             )
 
-        def quantize_h(c):
-            nc.vector.quantize_mx(out=h_codes[c][:].bitcast(FP8X4), scales=h_scales[c][:], in_=h_bf[c][:])
+        def sheet_words(c, a, b, count):
+            at = 2 * (size(c) * a + P * b)
+            return h_bf[c].bitcast(F32)[:, at : at + WIDE * count]
 
-        scaled, summed, new = {}, {}, {}
+        def turn_back(sheet, count, src, bank):
+            pairs = banks[bank][:, : WIDE * count]
+            for n in range(2 * count):
+                nc.tensor.transpose(pairs[:, P * n : P * (n + 1)], src[:, P * n : P * (n + 1)], identity[:])
+            nc.scalar.copy(
+                sheet_words(sheet[0], sheet[1], sheet[2], count).rearrange("p (b j u) -> p b j u", b=count, u=2),
+                pairs.rearrange("p (b u j) -> p b j u", b=count, u=2),
+            )
+
+        def residual_on_gpsimd(sheet, count):
+            c, a, b = sheet
+            entries = slice(P * b, P * (b + count))
+            nc.gpsimd.tensor_tensor(
+                sheet_words(c, a, b, count).bitcast(BF16).rearrange("p (g i t) -> p g t i", i=PACK, t=PACK),
+                measured[c, a][:, :, entries].rearrange("p t (g i) -> p g t i", i=PACK),
+                negated[c, a].rearrange("p (t j) -> p t j", t=PACK)[:, :, entries].rearrange("p t (g i) -> p g t i", i=PACK),
+                ALU.add,
+            )
+
+        def quantize_h(c, first, count):
+            nc.vector.quantize_mx(
+                out=h_codes[c][:, first : first + count].bitcast(FP8X4),
+                scales=h_scales[c][:, first : first + count],
+                in_=h_bf[c][:, PACK * first : PACK * (first + count)],
+            )
 
         def width(piece):
-            return CHUNK * (piece[2] + 1 - piece[1])
+            return EDGES[piece[2] + 1] - EDGES[piece[1]]
 
         def window(piece):
             i, first, last = piece
-            return maps[i][:].indirect(offsets[:, CHUNK * first // 16 : CHUNK * (last + 1) // 16])
+            return maps[i][:].indirect(offsets[:, EDGES[first] // 16 : EDGES[last + 1] // 16])
 
         def own(kind, piece, slot=None):
             return sb("%s%d_%d" % (kind, piece[0], piece[1]), [P, width(piece)], F32, slot)[:]
 
         def lead_back(piece, bank, dst):
-            i, first, last = piece
-            y = banks[bank][:, : width(piece)]
-            for c in range(last, first - 1, -1):
-                for a in range(PASSES):
+            i, c = piece[:2]
+            for a in range(PASSES):
+                for at in range(0, size(c), WIDE):
+                    count = min(WIDE, size(c) - at)
+                    entries = slice(size(c) * a + at, size(c) * a + at + count)
                     nc.tensor.matmul_mx(
-                        out=y[:, CHUNK * (c - first) : CHUNK * (c - first + 1)],
+                        out=banks[bank][:, at : at + count],
                         lhsT=b_words[i][:, P * a : P * (a + 1)].bitcast(FP8X4),
                         lhsT_scale=b_scales[4 * (a + 1) :, P * i : P * (i + 1)],
-                        rhs=h_codes[c][:, CHUNK * a : CHUNK * (a + 1)].bitcast(FP8X4),
-                        rhs_scale=h_scales[c][:, CHUNK * a : CHUNK * (a + 1)],
-                        start=(a == 0),
-                        stop=(a == PASSES - 1),
+                        rhs=h_codes[c][:, entries].bitcast(FP8X4),
+                        rhs_scale=h_scales[c][:, entries],
+                        start=(a == 0 and at == 0),
+                        stop=(a == PASSES - 1 and at + count == size(c)),
                     )
-            scaled[piece] = dst
-            nc.scalar.activation(dst, y, ACT.Copy, scale=steps[:, i : i + 1])
+            nc.scalar.activation(dst, banks[bank][:, : width(piece)], ACT.Copy, scale=steps[:, i : i + 1])
+            return dst
 
-        def gather_add(piece, dst):
-            summed[piece] = dst
-            nc.vector.tensor_tensor(dst, window(piece), scaled[piece], ALU.add)
+        def gather_add(piece, scaled, dst):
+            nc.vector.tensor_tensor(dst, window(piece), scaled, ALU.add)
+            return dst
 
-        def clamp(piece, dst):
-            new[piece] = dst
-            nc.scalar.activation(dst, summed[piece], ACT.Relu)
+        def clamp(summed, dst):
+            nc.scalar.activation(dst, summed, ACT.Relu)
+            return dst
 
-        def residual_on_gpsimd(a):
-            at = CHUNK * PACK * a
-            nc.gpsimd.tensor_tensor(
-                h_bf[3][:, at : at + CHUNK * PACK].rearrange("p (g i t) -> p g t i", i=PACK, t=PACK),
-                field_late[a][:, :, CHUNK:].rearrange("p t (g i) -> p g t i", i=PACK),
-                negated[3][:, at : at + CHUNK * PACK].rearrange("p (t g i) -> p g t i", t=PACK, i=PACK),
-                ALU.add,
-            )
-
-        def gather_chunk(i, c):
-            scaled[i, c, c] = scaled[i, 0, 1][:, CHUNK * c : CHUNK * (c + 1)]
-            gather_add((i, c, c), h_bf[3].bitcast(F32)[:, :CHUNK] if (i, c) == (2, 1) else own("summed", (i, c, c)))
-
-        def scatter(piece):
+        def scatter(piece, new):
             i, first, last = piece
-            nc.vector.tensor_copy(window(piece), new[piece])
-            if last == CHUNKS - 1:
+            nc.vector.tensor_copy(window(piece), new)
+            if last == D:
                 nc.sync.dma_start(out[P * i : P * (i + 1), :], maps[i][:])
+
+        parts = {A: slice(0, WIDE), B: slice(WIDE, WIDE + P)}
+
+        def gather_two(i, scaled, order):
+            summed = own("summed", (i, A, B))
+            for c in order:
+                gather_add((i, c, c), scaled[c], summed[:, parts[c]])
+            return summed
+
+        def clamp_two(i, summed):
+            new = own("new", (i, A, B))
+            for c in (A, B):
+                clamp(summed[:, parts[c]], new[:, parts[c]])
+            return new
 
         for a in range(PASSES):
             quantize_gm(a)
-        residual_on_vector(0, 0, 0)
-        residual_on_vector(0, 1, 4)
-        quantize_h(0)
-        residual_on_vector(1, 0, 2)
-        residual_on_vector(1, 1, 6)
-        negate_predictions(2, 0, 0)
-        negate_predictions(2, 1, 4)
+        residual_on_vector(A, 0, 0)
+        residual_on_vector(A, 1, 2)
+        quantize_h(A, 0, PASSES * WIDE)
+        residual_on_vector(B, 0, 4)
+        residual_on_vector(B, 1, 5)
+        scaled0 = lead_back((0, A, A), 2, own("scaled", (0, A, A), "first_slot"))
+        negate_wide(0, (0, 1))
+        negate_wide(1, (6, 4))
 
-        lead_back((0, 0, 0), 4, own("scaled", (0, 0, 0), "first_slot"))
-        gather_add((0, 0, 0), negated[3][:, PASS - P : PASS + P])
-        h_scales[1] = sb("h_scales1", [P, PASSES * CHUNK], U8, "first_slot")
-        quantize_h(1)
-        clamp((0, 0, 0), field_early[1, 1][:, 0, :])
-        scatter((0, 0, 0))
+        summed0 = gather_add((0, A, A), scaled0, negated[D, 0][:, :WIDE])
+        h_scales[B] = sb("h_scales1", [P, PASSES * P], U8, "first_slot")
+        quantize_h(B, 0, PASSES * P)
+        scatter((0, A, A), clamp(summed0, own("new", (0, A, A))))
 
-        held = [(0, 1, 1), (1, 1, 1)]
-        lead_back((1, 0, 0), 1, tile2_scaled[:, :CHUNK])
-        for n, piece in enumerate(held):
-            lead_back(piece, 2 + n, own("scaled", piece))
-        gather_add((1, 0, 0), new[0, 0, 0])
-        clamp((1, 0, 0), own("new", (1, 0, 0)))
-        for piece in held:
-            gather_add(piece, own("summed", piece))
-        scatter((1, 0, 0))
+        scaled1 = {
+            A: lead_back((1, A, A), 3, own("scaled", (1, A, A))),
+            B: lead_back((1, B, B), 2, own("scaled", (1, B, B))),
+        }
+        scaled0 = lead_back((0, B, B), 0, sheet_words(C, 0, 0, 1)[:, :P])
+        negate((D, 0, 0), 6)
+        negate((D, 0, 1), 5)
+        turn_negated((C, 0, 1), 3)
+        turn_negated((C, 1, 1), 0)
+        summed1 = gather_two(1, scaled1, (A, B))
+        summed0 = gather_add((0, B, B), scaled0, scaled1[A][:, :P])
+        residual_on_gpsimd((C, 0, 0), 1)
+        scatter((1, A, B), clamp_two(1, summed1))
 
-        negate_predictions(3, 0, 4)
-        lead_back((2, 0, 1), 4, tile2_scaled[:])
-        lead_back((3, 0, 1), 5, own("scaled", (3, 0, 1), "second_slot"))
-        negate_predictions(3, 1, 4)
+        scaled2 = {
+            A: lead_back((2, A, A), 1, own("scaled", (2, A, A))),
+            B: lead_back((2, B, B), 6, sheet_words(C, 1, 0, 1)[:, :P]),
+        }
+        add_field((C, 0, 1), 3, rounded_c[:, :WIDE])
+        turn_back((C, 0, 1), 1, rounded_c[:, :WIDE], 2)
+        negate((D, 0, 2), 1)
+        negate((D, 1, 0), 6)
+        for sheet, bank in (((D, 0, 1), 3), ((D, 0, 2), 1), ((D, 1, 0), 6)):
+            turn_negated(sheet, bank)
+        summed2 = gather_two(2, scaled2, (B, A))
+        lack = scaled2[B]
+        nc.scalar.activation(lack, summed0, ACT.Relu, scale=-1.0)
+        nc.vector.tensor_tensor(window((0, B, B)), summed0, lack, ALU.add)
+        residual_on_gpsimd((C, 1, 0), 1)
+        scatter((2, A, B), clamp_two(2, summed2))
 
-        for c, piece in enumerate(held):
-            gather_chunk(2, c)
-            clamp(piece, scaled[2, c, c])
-        new[2, 0, 1] = own("new", (2, 0, 1))
-        for c in range(2):
-            clamp((2, c, c), new[2, 0, 1][:, CHUNK * c : CHUNK * (c + 1)])
-        for piece in held + [(2, 0, 1)]:
-            scatter(piece)
+        scaled3 = {A: lead_back((3, A, A), 7, own("scaled", (3, A, A)))}
+        add_field((C, 1, 1), 0, rounded_c[:, WIDE:])
+        turn_back((C, 1, 1), 1, rounded_c[:, WIDE:], 2)
+        scaled3[B] = lead_back((3, B, B), 2, own("scaled", (3, B, B), "second_slot"))
+        negate((D, 1, 1), 0)
+        summed3 = gather_two(3, scaled3, (A, B))
+        h_scales[C] = sb("h_scales2", [P, PASSES * WIDE], U8, "second_slot")
+        quantize_h(C, 0, PASSES * WIDE)
+        residual_on_gpsimd((D, 0, 0), 1)
+        scatter((3, A, B), clamp_two(3, summed3))
+        negate((D, 1, 2), 2)
+        add_field((D, 0, 1), 3, rounded_d[:, :WIDE])
+        add_field((D, 0, 2), 1, rounded_d[:, WIDE:PASS])
 
-        residual_on_gpsimd(0)
-        units = [(2, a) for a in range(PASSES)]
-        for c, a in units:
-            turn_predictions(c, a)
-        for c, a in units:
-            finish_residual(c, a)
-            turn_back(c, a)
+        pieces = [(i, C, C) for i in range(TILES)]
+        scaled = [
+            lead_back(pieces[0], 4, own("scaled", pieces[0])),
+            lead_back(pieces[1], 5, own("scaled", pieces[1])),
+            lead_back(pieces[2], 7, sheet_words(D, 1, 1, 1)),
+        ]
+        turn_back((D, 0, 1), 2, rounded_d[:, :PASS], 3)
+        summed = [gather_add(pieces[i], scaled[i], own("summed", pieces[i])) for i in range(3)]
+        residual_on_gpsimd((D, 1, 1), 2)
+        scatter(pieces[0], clamp(summed[0], scaled[1]))
+        scatter(pieces[1], clamp(summed[1], own("new", pieces[1])))
+        add_field((D, 1, 0), 6, rounded_d[:, PASS:])
+        turn_back((D, 1, 0), 1, rounded_d[:, PASS:], 6)
+        h_scales[D] = sb("h_scales3", [P, PASSES * size(D)], U8, "field%d_%d" % (D, 1))
+        for a in range(PASSES):
+            quantize_h(D, size(D) * a, size(D))
+        last = gather_add(pieces[3], lead_back(pieces[3], 6, own("scaled", pieces[3])), negated[D, 1][:, PACK * size(D) - WIDE :])
+        scatter(pieces[2], clamp(summed[2], sheet_words(D, 0, 0, 1)))
+        scatter(pieces[3], clamp(last, own("new", pieces[3])))
 
-        for c in range(2):
-            gather_chunk(3, c)
-        h_scales[2] = sb("h_scales2", [P, PASSES * CHUNK], U8, "second_slot")
-        quantize_h(2)
-        residual_on_gpsimd(1)
-        new[3, 0, 1] = rounded[2, 1][:]
-        for c in range(2):
-            clamp((3, c, c), new[3, 0, 1][:, CHUNK * c : CHUNK * (c + 1)])
-        scatter((3, 0, 1))
-
-        middle = [(0, 2, 2), (1, 2, 2)]
-        for n, piece in enumerate(middle):
-            lead_back(piece, SUM_BANK[3, 1] + n, own("scaled", piece))
-        for piece in middle:
-            gather_add(piece, own("summed", piece))
-        clamp((0, 2, 2), own("new", (0, 2, 2)))
-        quantize_h(3)
-        clamp((1, 2, 2), h_bf[3][:].bitcast(F32)[:, :CHUNK])
-        for piece in middle:
-            scatter(piece)
-
-        late = [(0, 3, 3), (1, 3, 3), (2, 2, 3), (3, 2, 3)]
-        for bank, piece in enumerate(late):
-            lead_back(piece, bank, own("scaled", piece))
-        for piece in late:
-            gather_add(piece, own("summed", piece))
-            clamp(piece, own("new", piece))
-        for piece in late:
-            scatter(piece)
+        pieces = [(i, D, D) for i in range(TILES)]
+        scaled = [lead_back(pieces[i], (4, 5, 7)[i], own("scaled", pieces[i])) for i in range(3)]
+        summed = [gather_add(pieces[i], scaled[i], own("summed", pieces[i])) for i in range(3)]
+        scatter(pieces[0], clamp(summed[0], scaled[1]))
+        summed.append(gather_add(pieces[3], lead_back(pieces[3], 1, summed[0]), own("summed", pieces[3])))
+        for i in range(1, TILES):
+            scatter(pieces[i], clamp(summed[i], own("new", pieces[i])))

@@ -77,7 +77,7 @@ def tile_list_villa_survey_step_kernel(
             for a in range(PASSES):
                 negated[c, a] = sb("negated%d_%d" % (c, a), [P, PACK * size(c)], F32)[:]
         rounded_d = sb("rounded_d", [P, 3 * WIDE], F32)
-        rounded_c = sb("rounded_c", [P, PASS], F32)
+        rounded_c = sb("rounded_c", [P, WIDE], F32)
 
         nc.vector.memset(table_scales[:].bitcast(I32), 0)
         nc.vector.memset(step_rows[:], 0.0)
@@ -130,9 +130,9 @@ def tile_list_villa_survey_step_kernel(
         load_back_words(1)
         load_map(1)
         load_back_words(2)
+        load_map(2)
         load_field(C, 0)
         load_back_words(3)
-        load_map(2)
         load_field(C, 1)
         load_map(3)
         load_field(D, 0)
@@ -284,14 +284,12 @@ def tile_list_villa_survey_step_kernel(
 
         parts = {A: slice(0, WIDE), B: slice(WIDE, WIDE + P)}
 
-        def gather_two(i, scaled, order):
-            summed = own("summed", (i, A, B))
+        def gather_two(i, scaled, order, summed):
             for c in order:
                 gather_add((i, c, c), scaled[c], summed[:, parts[c]])
             return summed
 
-        def clamp_two(i, summed):
-            new = own("new", (i, A, B))
+        def clamp_two(i, summed, new):
             for c in (A, B):
                 clamp(summed[:, parts[c]], new[:, parts[c]])
             return new
@@ -312,50 +310,49 @@ def tile_list_villa_survey_step_kernel(
         quantize_h(B, 0, PASSES * P)
         scatter((0, A, A), clamp(summed0, own("new", (0, A, A))))
 
-        scaled1 = {
-            A: lead_back((1, A, A), 3, own("scaled", (1, A, A))),
-            B: lead_back((1, B, B), 2, own("scaled", (1, B, B))),
-        }
-        scaled0 = lead_back((0, B, B), 0, sheet_words(C, 0, 0, 1)[:, :P])
-        negate((D, 0, 0), 6)
-        negate((D, 0, 1), 5)
+        scaled1 = {A: lead_back((1, A, A), 3, own("scaled", (1, A, A)))}
+        scaled0 = lead_back((0, B, B), 0, own("scaled", (0, B, B)))
+        scaled1[B] = lead_back((1, B, B), 2, own("scaled", (1, B, B)))
+        negate((D, 0, 0), 5)
+        negate((D, 0, 1), 4)
+        summed0 = gather_add((0, B, B), scaled0, own("summed", (0, B, B)))
+        summed1 = gather_two(1, scaled1, (B, A), own("summed", (1, A, B)))
+        nc.scalar.activation(scaled1[B], summed0, ACT.Relu, scale=-1.0)
+        nc.vector.tensor_tensor(window((0, B, B)), summed0, scaled1[B], ALU.add)
         turn_negated((C, 0, 1), 3)
-        turn_negated((C, 1, 1), 0)
-        summed1 = gather_two(1, scaled1, (A, B))
-        summed0 = gather_add((0, B, B), scaled0, scaled1[A][:, :P])
-        residual_on_gpsimd((C, 0, 0), 1)
-        scatter((1, A, B), clamp_two(1, summed1))
 
+        new1 = own("new", (1, A, B))
         scaled2 = {
-            A: lead_back((2, A, A), 1, own("scaled", (2, A, A))),
-            B: lead_back((2, B, B), 6, sheet_words(C, 1, 0, 1)[:, :P]),
+            B: lead_back((2, B, B), 6, new1[:, parts[B]]),
+            A: lead_back((2, A, A), 1, sheet_words(C, 0, 0, 1)),
         }
-        add_field((C, 0, 1), 3, rounded_c[:, :WIDE])
-        turn_back((C, 0, 1), 1, rounded_c[:, :WIDE], 2)
-        negate((D, 0, 2), 1)
-        negate((D, 1, 0), 6)
-        for sheet, bank in (((D, 0, 1), 3), ((D, 0, 2), 1), ((D, 1, 0), 6)):
-            turn_negated(sheet, bank)
-        summed2 = gather_two(2, scaled2, (B, A))
-        lack = scaled2[B]
-        nc.scalar.activation(lack, summed0, ACT.Relu, scale=-1.0)
-        nc.vector.tensor_tensor(window((0, B, B)), summed0, lack, ALU.add)
-        residual_on_gpsimd((C, 1, 0), 1)
-        scatter((2, A, B), clamp_two(2, summed2))
+        clamp(summed1[:, parts[A]], new1[:, parts[A]])
+        turn_negated((D, 0, 1), 1)
+        summed2 = gather_two(2, scaled2, (B, A), own("summed", (2, A, B)))
+        clamp(summed1[:, parts[B]], new1[:, parts[B]])
+        residual_on_gpsimd((C, 0, 0), 1)
+        residual_on_gpsimd((C, 1, 0), 2)
+        scatter((1, A, B), new1)
+        scatter((2, A, B), clamp_two(2, summed2, own("new", (2, A, B))))
+        add_field((C, 0, 1), 3, rounded_c[:])
+        turn_back((C, 0, 1), 1, rounded_c[:], 2)
 
-        scaled3 = {A: lead_back((3, A, A), 7, own("scaled", (3, A, A)))}
-        add_field((C, 1, 1), 0, rounded_c[:, WIDE:])
-        turn_back((C, 1, 1), 1, rounded_c[:, WIDE:], 2)
-        scaled3[B] = lead_back((3, B, B), 2, own("scaled", (3, B, B), "second_slot"))
+        scaled3 = {
+            B: lead_back((3, B, B), 0, own("scaled", (3, B, B), "second_slot")),
+            A: lead_back((3, A, A), 7, own("scaled", (3, A, A))),
+        }
+        for sheet, bank in (((D, 0, 2), 3), ((D, 1, 0), 2)):
+            negate(sheet, bank)
+            turn_negated(sheet, bank)
         negate((D, 1, 1), 0)
-        summed3 = gather_two(3, scaled3, (A, B))
+        negate((D, 1, 2), 7)
+        summed3 = gather_two(3, scaled3, (B, A), negated[C, 1][:, : WIDE + P])
         h_scales[C] = sb("h_scales2", [P, PASSES * WIDE], U8, "second_slot")
         quantize_h(C, 0, PASSES * WIDE)
         residual_on_gpsimd((D, 0, 0), 1)
-        scatter((3, A, B), clamp_two(3, summed3))
-        negate((D, 1, 2), 2)
-        add_field((D, 0, 1), 3, rounded_d[:, :WIDE])
-        add_field((D, 0, 2), 1, rounded_d[:, WIDE:PASS])
+        scatter((3, A, B), clamp_two(3, summed3, own("new", (3, A, B))))
+        add_field((D, 0, 1), 1, rounded_d[:, :WIDE])
+        add_field((D, 0, 2), 3, rounded_d[:, WIDE:PASS])
 
         pieces = [(i, C, C) for i in range(TILES)]
         scaled = [
@@ -363,22 +360,22 @@ def tile_list_villa_survey_step_kernel(
             lead_back(pieces[1], 5, own("scaled", pieces[1])),
             lead_back(pieces[2], 7, sheet_words(D, 1, 1, 1)),
         ]
-        turn_back((D, 0, 1), 2, rounded_d[:, :PASS], 3)
+        turn_back((D, 0, 1), 2, rounded_d[:, :PASS], 7)
         summed = [gather_add(pieces[i], scaled[i], own("summed", pieces[i])) for i in range(3)]
         residual_on_gpsimd((D, 1, 1), 2)
         scatter(pieces[0], clamp(summed[0], scaled[1]))
         scatter(pieces[1], clamp(summed[1], own("new", pieces[1])))
-        add_field((D, 1, 0), 6, rounded_d[:, PASS:])
-        turn_back((D, 1, 0), 1, rounded_d[:, PASS:], 6)
+        add_field((D, 1, 0), 2, rounded_d[:, PASS:])
+        turn_back((D, 1, 0), 1, rounded_d[:, PASS:], 7)
         h_scales[D] = sb("h_scales3", [P, PASSES * size(D)], U8, "field%d_%d" % (D, 1))
         for a in range(PASSES):
             quantize_h(D, size(D) * a, size(D))
-        last = gather_add(pieces[3], lead_back(pieces[3], 6, own("scaled", pieces[3])), negated[D, 1][:, PACK * size(D) - WIDE :])
+        last = gather_add(pieces[3], lead_back(pieces[3], 7, own("scaled", pieces[3])), negated[D, 1][:, PACK * size(D) - WIDE :])
         scatter(pieces[2], clamp(summed[2], sheet_words(D, 0, 0, 1)))
         scatter(pieces[3], clamp(last, own("new", pieces[3])))
 
         pieces = [(i, D, D) for i in range(TILES)]
-        scaled = [lead_back(pieces[i], (4, 5, 7)[i], own("scaled", pieces[i])) for i in range(3)]
+        scaled = [lead_back(pieces[i], (4, 5, 3)[i], own("scaled", pieces[i])) for i in range(3)]
         summed = [gather_add(pieces[i], scaled[i], own("summed", pieces[i])) for i in range(3)]
         scatter(pieces[0], clamp(summed[0], scaled[1]))
         summed.append(gather_add(pieces[3], lead_back(pieces[3], 1, summed[0]), own("summed", pieces[3])))

@@ -251,6 +251,12 @@ def tile_list_villa_survey_step_kernel(
             return sb("%s%d_%d" % (kind, piece[0], piece[1]), [P, width(piece)], F32, slot)[:]
 
         def lead_back(piece, bank, dst):
+            product(piece, bank)
+            i = piece[0]
+            nc.scalar.activation(dst, banks[bank][:, : width(piece)], ACT.Copy, scale=steps[:, i : i + 1])
+            return dst
+
+        def product(piece, bank):
             i, c = piece[:2]
             for a in range(PASSES):
                 for at in range(0, size(c), WIDE):
@@ -265,8 +271,6 @@ def tile_list_villa_survey_step_kernel(
                         start=(a == 0 and at == 0),
                         stop=(a == PASSES - 1 and at + count == size(c)),
                     )
-            nc.scalar.activation(dst, banks[bank][:, : width(piece)], ACT.Copy, scale=steps[:, i : i + 1])
-            return dst
 
         def gather_add(piece, scaled, dst):
             nc.vector.tensor_tensor(dst, window(piece), scaled, ALU.add)
@@ -306,16 +310,19 @@ def tile_list_villa_survey_step_kernel(
         negate_wide(1, (6, 4))
 
         summed0 = gather_add((0, A, A), scaled0, negated[D, 0][:, :WIDE])
+        picked = own("picked", (0, B, B))
+        nc.vector.tensor_copy(picked, window((0, B, B)))
         h_scales[B] = sb("h_scales1", [P, PASSES * P], U8, "first_slot")
         quantize_h(B, 0, PASSES * P)
         scatter((0, A, A), clamp(summed0, own("new", (0, A, A))))
 
         scaled1 = {A: lead_back((1, A, A), 3, own("scaled", (1, A, A)))}
-        scaled0 = lead_back((0, B, B), 0, own("scaled", (0, B, B)))
+        product((0, B, B), 0)
         scaled1[B] = lead_back((1, B, B), 2, own("scaled", (1, B, B)))
         negate((D, 0, 0), 5)
         negate((D, 0, 1), 4)
-        summed0 = gather_add((0, B, B), scaled0, own("summed", (0, B, B)))
+        summed0 = own("summed", (0, B, B))
+        nc.vector.scalar_tensor_tensor(summed0, banks[0][:, :P], steps[:, 0:1], picked, ALU.mult, ALU.add)
         summed1 = gather_two(1, scaled1, (B, A), own("summed", (1, A, B)))
         nc.scalar.activation(scaled1[B], summed0, ACT.Relu, scale=-1.0)
         nc.vector.tensor_tensor(window((0, B, B)), summed0, scaled1[B], ALU.add)

@@ -26,6 +26,7 @@ BANKS = 8
 A, B, C, D = range(4)
 EDGES = (0, 256, 384, 640, 1024)
 WIDE = 2 * P
+SCALAR_SHARE = (44, 66)
 OVERLAP = 64
 
 
@@ -51,7 +52,7 @@ def tile_list_villa_survey_step_kernel(
         b_words = [sb("b_words%d" % i, [P, PASSES * P], I32) for i in range(TILES)]
         steps = sb("steps", [P, TILES], F32)
         maps = [sb("map%d" % i, [P, T], F32) for i in range(TILES)]
-        gm_raw = [[sb("gm_raw%d_%d" % (a, n), [P, PACK, WIDE], F32) for n in range(2)] for a in range(PASSES)]
+        gm_raw = sb("gm_raw", [P, PACK * H], F32)
         woven = sb("woven", [P, 2 * PASS * PACK - OVERLAP], BF16)
         gm_bf = [woven[:, PASS * PACK - OVERLAP :], woven[:, : PASS * PACK]]
         gm_codes = [sb("gm_codes%d" % a, [P, PASS], U32) for a in range(PASSES)]
@@ -65,14 +66,11 @@ def tile_list_villa_survey_step_kernel(
             h_codes[c] = sb("h_codes%d" % c, [P, PASSES * size(c)], U32)
         h_scales[A] = sb("h_scales0", [P, PASSES * size(A)], U8)
         h_bf[A] = sb("h_early", [P, PASSES * PACK * size(A)], BF16)[:]
-        h_bf[B] = h_bf[A][:, : PASSES * PACK * size(B)]
+        h_bf[B] = h_bf[A][:, PACK * size(A) :]
         h_late = sb("h_late", [P, PASSES * PACK * (size(C) + size(D)) - PASS], BF16)
         h_bf[C] = h_late[:, : PASSES * PACK * size(C)]
         h_bf[D] = h_late[:, PASSES * PACK * size(C) - PASS :]
         measured, negated = {}, {}
-        for c in (A, B, C, D):
-            for a in range(PASSES):
-                measured[c, a] = sb("field%d_%d" % (c, a), [P, PACK, size(c)], F32)
         for c in (C, D):
             for a in range(PASSES):
                 negated[c, a] = sb("negated%d_%d" % (c, a), [P, PACK * size(c)], F32)[:]
@@ -84,14 +82,12 @@ def tile_list_villa_survey_step_kernel(
         nc.vector.memset(b_scales[:].bitcast(I32), 0)
         make_identity(nc, identity[:])
 
-        def load_gm(a):
-            for n in range(2):
-                columns = gm[:, PASS * a + WIDE * n : PASS * a + WIDE * (n + 1)]
-                nc.sync.dma_start(gm_raw[a][n][:], columns.rearrange("(p j) c -> p j c", j=PACK))
-
-        def load_field(c, a):
-            rows = field[PASS * a : PASS * (a + 1), EDGES[c] : EDGES[c + 1]]
-            nc.sync.dma_start(measured[c, a][:], rows.rearrange("(p t) j -> p t j", t=PACK))
+        def load_field(first, last, a):
+            dst = sb("field%d_%d" % (first, a), [P, PACK, EDGES[last + 1] - EDGES[first]], F32)
+            rows = field[PASS * a : PASS * (a + 1), EDGES[first] : EDGES[last + 1]]
+            nc.sync.dma_start(dst[:], rows.rearrange("(p t) j -> p t j", t=PACK))
+            for c in range(first, last + 1):
+                measured[c, a] = dst[:, :, EDGES[c] - EDGES[first] : EDGES[c + 1] - EDGES[first]]
 
         def load_back_words(i):
             nc.sync.dma_start(
@@ -104,49 +100,45 @@ def tile_list_villa_survey_step_kernel(
 
         nc.sync.dma_start(offsets[:], offs)
         words = tab_words[0].rearrange("p t i -> p (t i)").bitcast(I32)
-        nc.sync.dma_start(table_words[:, : T // 2], words[:, : T // 2])
+        nc.sync.dma_start(table_words[:], words)
         for quad in range(QUADS):
             nc.sync.dma_start(
                 table_scales[32 * quad : 32 * quad + 4, :].bitcast(I32),
                 tab_scales[0, 4 * quad : 4 * quad + 4, :].bitcast(I32),
             )
-        nc.sync.dma_start(table_words[:, T // 2 :], words[:, T // 2 :])
         nc.sync.dma_start(step_rows[:TILES, :], step.rearrange("(i p) -> i p", p=P))
         nc.tensor.transpose(banks[-1][:, :P], step_rows[:], identity[:])
         nc.scalar.copy(steps[:], banks[-1][:, :TILES])
-        load_gm(0)
+        nc.sync.dma_start(gm_raw[:], gm.rearrange("(p j) c -> p (j c)", j=PACK))
         for quad in range(QUADS):
             nc.sync.dma_start(
                 b_scales[32 * quad + 4 : 32 * quad + 12, :].bitcast(I32),
                 back_scales[:, 4 * quad : 4 * quad + 4, :].bitcast(I32),
             )
-        load_gm(1)
-        load_field(A, 0)
-        load_field(A, 1)
+        load_field(A, B, 0)
+        load_field(A, A, 1)
         load_back_words(0)
-        load_field(B, 0)
-        load_field(B, 1)
+        load_field(B, B, 1)
         load_map(0)
         load_back_words(1)
         load_map(1)
         load_back_words(2)
         load_map(2)
-        load_field(C, 0)
+        load_field(C, C, 0)
+        load_field(C, C, 1)
         load_back_words(3)
-        load_field(C, 1)
         load_map(3)
-        load_field(D, 0)
-        load_field(D, 1)
+        load_field(D, D, 0)
+        load_field(D, D, 1)
 
-        nc.vector.tensor_copy(v_scales[:], table_scales[:].indirect(offsets[:]))
         nc.vector.tensor_copy(v_words[:], table_words[:].bitcast(U32).indirect(offsets[:]))
+        nc.vector.tensor_copy(v_scales[:], table_scales[:].indirect(offsets[:]))
 
         def quantize_gm(a):
             dst = gm_bf[a].rearrange("p (t m j) -> p m j t", t=PACK, j=PACK)
-            for n in range(2):
-                weave = nc.vector.tensor_copy if (a, n) == (PASSES - 1, 1) else nc.scalar.copy
-                src = gm_raw[a][n][:].rearrange("p j (m t) -> p m j t", t=PACK)
-                weave(dst[:, P // 2 * n : P // 2 * (n + 1)], src)
+            src = gm_raw[:].rearrange("p (j a m t) -> p a m j t", j=PACK, a=PASSES, t=PACK)[:, a]
+            nc.scalar.copy(dst[:, : SCALAR_SHARE[a]], src[:, : SCALAR_SHARE[a]])
+            nc.vector.tensor_copy(dst[:, SCALAR_SHARE[a] :], src[:, SCALAR_SHARE[a] :])
             nc.vector.quantize_mx(out=gm_codes[a][:].bitcast(FP8X4), scales=gm_scales[a][:], in_=gm_bf[a])
 
         def predict(dst, a, t, first, count):
@@ -302,7 +294,8 @@ def tile_list_villa_survey_step_kernel(
             quantize_gm(a)
         residual_on_vector(A, 0, 0)
         residual_on_vector(A, 1, 2)
-        quantize_h(A, 0, PASSES * WIDE)
+        for a in range(PASSES):
+            quantize_h(A, WIDE * a, WIDE)
         residual_on_vector(B, 0, 4)
         residual_on_vector(B, 1, 5)
         scaled0 = lead_back((0, A, A), 2, own("scaled", (0, A, A), "first_slot"))

@@ -26,8 +26,8 @@ BANKS = 8
 A, B, C, D = range(4)
 EDGES = (0, 256, 384, 640, 1024)
 WIDE = 2 * P
-SCALAR_SHARE = (44, 66)
-OVERLAP = 64
+SCALAR_SHARE = (40, 66)
+WARM_UPS = 3
 
 
 def tile_list_villa_survey_step_kernel(
@@ -53,8 +53,7 @@ def tile_list_villa_survey_step_kernel(
         steps = sb("steps", [P, TILES], F32)
         maps = [sb("map%d" % i, [P, T], F32) for i in range(TILES)]
         gm_raw = sb("gm_raw", [P, PACK * H], F32)
-        woven = sb("woven", [P, 2 * PASS * PACK - OVERLAP], BF16)
-        gm_bf = [woven[:, PASS * PACK - OVERLAP :], woven[:, : PASS * PACK]]
+        gm_bf = [sb("gm_bf%d" % a, [P, PASS * PACK], BF16)[:] for a in range(PASSES)]
         gm_codes = [sb("gm_codes%d" % a, [P, PASS], U32) for a in range(PASSES)]
         gm_scales = [sb("gm_scales%d" % a, [P, PASS], U8) for a in range(PASSES)]
         v_words = sb("v_words", [P, S], U32)
@@ -66,7 +65,7 @@ def tile_list_villa_survey_step_kernel(
             h_codes[c] = sb("h_codes%d" % c, [P, PASSES * size(c)], U32)
         h_scales[A] = sb("h_scales0", [P, PASSES * size(A)], U8)
         h_bf[A] = sb("h_early", [P, PASSES * PACK * size(A)], BF16)[:]
-        h_bf[B] = h_bf[A][:, PACK * size(A) :]
+        h_bf[B] = h_bf[A][:, : PACK * size(A)]
         h_late = sb("h_late", [P, PASSES * PACK * (size(C) + size(D)) - PASS], BF16)
         h_bf[C] = h_late[:, : PASSES * PACK * size(C)]
         h_bf[D] = h_late[:, PASSES * PACK * size(C) - PASS :]
@@ -134,12 +133,22 @@ def tile_list_villa_survey_step_kernel(
         nc.vector.tensor_copy(v_words[:], table_words[:].bitcast(U32).indirect(offsets[:]))
         nc.vector.tensor_copy(v_scales[:], table_scales[:].indirect(offsets[:]))
 
-        def quantize_gm(a):
+        for n in range(WARM_UPS):
+            nc.tensor.matmul_mx(
+                out=banks[-1][:],
+                lhsT=v_words[:, :P].bitcast(FP8X4),
+                lhsT_scale=v_scales[:, :P],
+                rhs=v_words[:, :PASS].bitcast(FP8X4),
+                rhs_scale=v_scales[:, :PASS],
+                start=True,
+                stop=True,
+            )
+
+        def weave_gm(a):
             dst = gm_bf[a].rearrange("p (t m j) -> p m j t", t=PACK, j=PACK)
             src = gm_raw[:].rearrange("p (j a m t) -> p a m j t", j=PACK, a=PASSES, t=PACK)[:, a]
             nc.scalar.copy(dst[:, : SCALAR_SHARE[a]], src[:, : SCALAR_SHARE[a]])
             nc.vector.tensor_copy(dst[:, SCALAR_SHARE[a] :], src[:, SCALAR_SHARE[a] :])
-            nc.vector.quantize_mx(out=gm_codes[a][:].bitcast(FP8X4), scales=gm_scales[a][:], in_=gm_bf[a])
 
         def predict(dst, a, t, first, count):
             nc.tensor.matmul_mx(
@@ -152,18 +161,18 @@ def tile_list_villa_survey_step_kernel(
                 stop=True,
             )
 
-        def residual_on_vector(c, a, first_bank):
-            for b in range(size(c) // P):
-                pred = banks[first_bank + b][:].rearrange("p (t j) -> p t j", t=PACK)
-                for t in range(PACK):
-                    predict(pred[:, t, :], a, t, EDGES[c] + P * b, P)
-                at = PACK * (size(c) * a + P * b)
-                nc.vector.tensor_tensor(
-                    h_bf[c][:, at : at + PASS].rearrange("p (g i t) -> p g t i", i=PACK, t=PACK),
-                    measured[c, a][:, :, P * b : P * (b + 1)].rearrange("p t (g i) -> p g t i", i=PACK),
-                    pred.rearrange("p t (g i) -> p g t i", i=PACK),
-                    ALU.subtract,
-                )
+        def residual_on_vector(sheet, bank):
+            c, a, b = sheet
+            pred = banks[bank][:].rearrange("p (t j) -> p t j", t=PACK)
+            for t in range(PACK):
+                predict(pred[:, t, :], a, t, EDGES[c] + P * b, P)
+            at = PACK * (size(c) * a + P * b)
+            nc.vector.tensor_tensor(
+                h_bf[c][:, at : at + PASS].rearrange("p (g i t) -> p g t i", i=PACK, t=PACK),
+                measured[c, a][:, :, P * b : P * (b + 1)].rearrange("p t (g i) -> p g t i", i=PACK),
+                pred.rearrange("p t (g i) -> p g t i", i=PACK),
+                ALU.subtract,
+            )
 
         def negate_wide(a, two_banks):
             for u in range(2):
@@ -291,13 +300,16 @@ def tile_list_villa_survey_step_kernel(
             return new
 
         for a in range(PASSES):
-            quantize_gm(a)
-        residual_on_vector(A, 0, 0)
-        residual_on_vector(A, 1, 2)
+            weave_gm(a)
+        for a in range(PASSES):
+            nc.vector.quantize_mx(out=gm_codes[a][:].bitcast(FP8X4), scales=gm_scales[a][:], in_=gm_bf[a])
+        for b in range(2):
+            for a in range(PASSES):
+                residual_on_vector((A, a, b), 2 * a + b)
         for a in range(PASSES):
             quantize_h(A, WIDE * a, WIDE)
-        residual_on_vector(B, 0, 4)
-        residual_on_vector(B, 1, 5)
+        residual_on_vector((B, 0, 0), 4)
+        residual_on_vector((B, 1, 0), 5)
         scaled0 = lead_back((0, A, A), 2, own("scaled", (0, A, A), "first_slot"))
         negate_wide(0, (0, 1))
         negate_wide(1, (6, 4))

from contextlib import ExitStack

import concourse.mybir as mybir
from concourse.masks import make_identity

K, H, T, S = 512, 1024, 2048, 1024
FLOPS = 2 * K * H * S + 2 * H * K * S

F32 = mybir.dt.float32
BF16 = mybir.dt.bfloat16
I32 = mybir.dt.int32
U32 = mybir.dt.uint32
U16 = mybir.dt.uint16
U8 = mybir.dt.uint8
FP8X4 = mybir.dt.float8_e4m3fn_x4
ALU = mybir.AluOpType
ACT = mybir.ActivationFunctionType

P = 128
PACK = 4
PASS = P * PACK
PASSES = H // PASS
TILES = K // P
QUADS = 4
BANKS = 8
A, B, C, D = range(4)
EDGES = (0, 256, 384, 640, 1024)
WIDE = 2 * P
SCALAR_SHARE = (40, 66)
WARM_UPS = 3


def tile_list_villa_survey_step_kernel(
    tc, tab_words, tab_scales, offs, gT, gm, field, back_words, back_scales, step, out
):
    nc = tc.nc
    with ExitStack() as ctx:
        keep = ctx.enter_context(tc.tile_pool(name="keep", bufs=1))
        psum = ctx.enter_context(tc.psum_pool(name="psum", bufs=1))
        banks = [psum.tile([P, PASS], F32, name="bank%d" % n, tag="bank%d" % n) for n in range(BANKS)]

        def sb(name, shape, dtype, slot=None):
            return keep.tile(shape, dtype, name=name, tag=slot or name, align_bytes=64)

        def size(c):
            return EDGES[c + 1] - EDGES[c]

        offsets = keep.tile([P, S // 16], U16, name="offsets")
        table_scales = sb("table_scales", [P, T], U8)
        table_words = sb("table_words", [P, T], I32)
        b_scales = sb("b_scales", [P, K], U8)
        b_words = [sb("b_words%d" % i, [P, PASSES * P], I32) for i in range(TILES)]
        steps = sb("steps", [P, TILES], F32)
        maps = [sb("map%d" % i, [P, T], F32) for i in range(TILES)]
        gm_raw = sb("gm_raw", [P, PACK * H], F32)
        gm_bf = [sb("gm_bf%d" % a, [P, PASS * PACK], BF16)[:] for a in range(PASSES)]
        gm_codes = [sb("gm_codes%d" % a, [P, PASS], U32) for a in range(PASSES)]
        gm_scales = [sb("gm_scales%d" % a, [P, PASS], U8) for a in range(PASSES)]
        v_words = sb("v_words", [P, S], U32)
        v_scales = sb("v_scales", [P, S], U8)
        identity = sb("identity", [P, P], F32)
        step_rows = sb("step_rows", [P, P], F32)
        h_bf, h_codes, h_scales = {}, {}, {}
        for c in (A, B, C, D):
            h_codes[c] = sb("h_codes%d" % c, [P, PASSES * size(c)], U32)
        h_scales[A] = sb("h_scales0", [P, PASSES * size(A)], U8)
        h_bf[A] = sb("h_early", [P, PASSES * PACK * size(A)], BF16)[:]
        h_bf[B] = h_bf[A][:, : PACK * size(A)]
        h_late = sb("h_late", [P, PASSES * PACK * (size(C) + size(D)) - PASS], BF16)
        h_bf[C] = h_late[:, : PASSES * PACK * size(C)]
        h_bf[D] = h_late[:, PASSES * PACK * size(C) - PASS :]
        measured, negated = {}, {}
        for c in (C, D):
            for a in range(PASSES):
                negated[c, a] = sb("negated%d_%d" % (c, a), [P, PACK * size(c)], F32)[:]
        rounded_d = sb("rounded_d", [P, 3 * WIDE], F32)
        rounded_c = sb("rounded_c", [P, WIDE], F32)

        nc.vector.memset(table_scales[:].bitcast(I32), 0)
        nc.vector.memset(step_rows[:], 0.0)
        nc.vector.memset(b_scales[:].bitcast(I32), 0)
        make_identity(nc, identity[:])

        def load_field(first, last, a):
            dst = sb("field%d_%d" % (first, a), [P, PACK, EDGES[last + 1] - EDGES[first]], F32)
            rows = field[PASS * a : PASS * (a + 1), EDGES[first] : EDGES[last + 1]]
            nc.sync.dma_start(dst[:], rows.rearrange("(p t) j -> p t j", t=PACK))
            for c in range(first, last + 1):
                measured[c, a] = dst[:, :, EDGES[c] - EDGES[first] : EDGES[c + 1] - EDGES[first]]

        def load_back_words(i):
            nc.sync.dma_start(
                b_words[i][:].rearrange("p (a c) -> p a c", a=PASSES),
                back_words.rearrange("a p c i -> p a (c i)").bitcast(I32)[:, :, P * i : P * (i + 1)],
            )

        def load_map(i):
            nc.sync.dma_start(maps[i][:], gT[P * i : P * (i + 1), :])

        nc.sync.dma_start(offsets[:], offs)
        words = tab_words[0].rearrange("p t i -> p (t i)").bitcast(I32)
        nc.sync.dma_start(table_words[:], words)
        for quad in range(QUADS):
            nc.sync.dma_start(
                table_scales[32 * quad : 32 * quad + 4, :].bitcast(I32),
                tab_scales[0, 4 * quad : 4 * quad + 4, :].bitcast(I32),
            )
        nc.sync.dma_start(step_rows[:TILES, :], step.rearrange("(i p) -> i p", p=P))
        nc.tensor.transpose(banks[-1][:, :P], step_rows[:], identity[:])
        nc.scalar.copy(steps[:], banks[-1][:, :TILES])
        nc.sync.dma_start(gm_raw[:], gm.rearrange("(p j) c -> p (j c)", j=PACK))
        for quad in range(QUADS):
            nc.sync.dma_start(
                b_scales[32 * quad + 4 : 32 * quad + 12, :].bitcast(I32),
                back_scales[:, 4 * quad : 4 * quad + 4, :].bitcast(I32),
            )
        load_field(A, B, 0)
        load_field(A, A, 1)
        load_back_words(0)
        load_field(B, B, 1)
        load_map(0)
        load_back_words(1)
        load_map(1)
        load_back_words(2)
        load_map(2)
        load_field(C, C, 0)
        load_field(C, C, 1)
        load_back_words(3)
        load_map(3)
        load_field(D, D, 0)
        load_field(D, D, 1)

        nc.vector.tensor_copy(v_words[:], table_words[:].bitcast(U32).indirect(offsets[:]))
        nc.vector.tensor_copy(v_scales[:], table_scales[:].indirect(offsets[:]))

        for n in range(WARM_UPS):
            nc.tensor.matmul_mx(
                out=banks[-1][:],
                lhsT=v_words[:, :P].bitcast(FP8X4),
                lhsT_scale=v_scales[:, :P],
                rhs=v_words[:, :PASS].bitcast(FP8X4),
                rhs_scale=v_scales[:, :PASS],
                start=True,
                stop=True,
            )

        def weave_gm(a):
            dst = gm_bf[a].rearrange("p (t m j) -> p m j t", t=PACK, j=PACK)
            src = gm_raw[:].rearrange("p (j a m t) -> p a m j t", j=PACK, a=PASSES, t=PACK)[:, a]
            nc.scalar.copy(dst[:, : SCALAR_SHARE[a]], src[:, : SCALAR_SHARE[a]])
            nc.vector.tensor_copy(dst[:, SCALAR_SHARE[a] :], src[:, SCALAR_SHARE[a] :])

        def predict(dst, a, t, first, count):
            nc.tensor.matmul_mx(
                out=dst,
                lhsT=gm_codes[a][:, P * t : P * (t + 1)].bitcast(FP8X4),
                lhsT_scale=gm_scales[a][:, P * t : P * (t + 1)],
                rhs=v_words[:, first : first + count].bitcast(FP8X4),
                rhs_scale=v_scales[:, first : first + count],
                start=True,
                stop=True,
            )

        def residual_on_vector(sheet, bank):
            c, a, b = sheet
            pred = banks[bank][:].rearrange("p (t j) -> p t j", t=PACK)
            for t in range(PACK):
                predict(pred[:, t, :], a, t, EDGES[c] + P * b, P)
            at = PACK * (size(c) * a + P * b)
            nc.vector.tensor_tensor(
                h_bf[c][:, at : at + PASS].rearrange("p (g i t) -> p g t i", i=PACK, t=PACK),
                measured[c, a][:, :, P * b : P * (b + 1)].rearrange("p t (g i) -> p g t i", i=PACK),
                pred.rearrange("p t (g i) -> p g t i", i=PACK),
                ALU.subtract,
            )

        def negate_wide(a, two_banks):
            for u in range(2):
                bank = banks[two_banks[u]]
                for e in range(2):
                    predict(bank[:, WIDE * e : WIDE * (e + 1)], a, 2 * u + e, EDGES[C], WIDE)
                nc.scalar.activation(negated[C, a][:, PASS * u : PASS * (u + 1)], bank[:], ACT.Copy, scale=-1.0)

        def negate(sheet, bank):
            c, a, b = sheet
            pred = banks[bank][:].rearrange("p (t j) -> p t j", t=PACK)
            for t in range(PACK):
                predict(pred[:, t, :], a, t, EDGES[c] + P * b, P)
            dst = negated[c, a].rearrange("p (t j) -> p t j", t=PACK)[:, :, P * b : P * (b + 1)]
            nc.scalar.activation(dst, pred, ACT.Copy, scale=-1.0)

        def turn_negated(sheet, bank):
            c, a, b = sheet
            for t in range(PACK):
                at = size(c) * t + P * b
                nc.tensor.matmul(
                    banks[bank][:, P * t : P * (t + 1)], negated[c, a][:, at : at + P], identity[:],
                    start=(t == 0), stop=False, is_transpose=True,
                )

        def add_field(sheet, bank, dst):
            c, a, b = sheet
            for t in range(PACK):
                nc.tensor.matmul(
                    banks[bank][:, P * t : P * (t + 1)], measured[c, a][:, t, P * b : P * (b + 1)], identity[:],
                    start=False, stop=(t == PACK - 1), is_transpose=True,
                )
            nc.scalar.activation(
                dst.bitcast(BF16).rearrange("j (u p e) -> j u p e", u=2, e=2),
                banks[bank][:].rearrange("j (u e p) -> j u p e", u=2, e=2),
                ACT.Copy,
            )

        def sheet_words(c, a, b, count):
            at = 2 * (size(c) * a + P * b)
            return h_bf[c].bitcast(F32)[:, at : at + WIDE * count]

        def turn_back(sheet, count, src, bank):
            pairs = banks[bank][:, : WIDE * count]
            for n in range(2 * count):
                nc.tensor.transpose(pairs[:, P * n : P * (n + 1)], src[:, P * n : P * (n + 1)], identity[:])
            nc.scalar.copy(
                sheet_words(sheet[0], sheet[1], sheet[2], count).rearrange("p (b j u) -> p b j u", b=count, u=2),
                pairs.rearrange("p (b u j) -> p b j u", b=count, u=2),
            )

        def residual_on_gpsimd(sheet, count):
            c, a, b = sheet
            entries = slice(P * b, P * (b + count))
            nc.gpsimd.tensor_tensor(
                sheet_words(c, a, b, count).bitcast(BF16).rearrange("p (g i t) -> p g t i", i=PACK, t=PACK),
                measured[c, a][:, :, entries].rearrange("p t (g i) -> p g t i", i=PACK),
                negated[c, a].rearrange("p (t j) -> p t j", t=PACK)[:, :, entries].rearrange("p t (g i) -> p g t i", i=PACK),
                ALU.add,
            )

        def quantize_h(c, first, count):
            nc.vector.quantize_mx(
                out=h_codes[c][:, first : first + count].bitcast(FP8X4),
                scales=h_scales[c][:, first : first + count],
                in_=h_bf[c][:, PACK * first : PACK * (first + count)],
            )

        def width(piece):
            return EDGES[piece[2] + 1] - EDGES[piece[1]]

        def window(piece):
            i, first, last = piece
            return maps[i][:].indirect(offsets[:, EDGES[first] // 16 : EDGES[last + 1] // 16])

        def own(kind, piece, slot=None):
            return sb("%s%d_%d" % (kind, piece[0], piece[1]), [P, width(piece)], F32, slot)[:]

        def lead_back(piece, bank, dst):
            product(piece, bank)
            i = piece[0]
            nc.scalar.activation(dst, banks[bank][:, : width(piece)], ACT.Copy, scale=steps[:, i : i + 1])
            return dst

        def product(piece, bank):
            i, c = piece[:2]
            for a in range(PASSES):
                for at in range(0, size(c), WIDE):
                    count = min(WIDE, size(c) - at)
                    entries = slice(size(c) * a + at, size(c) * a + at + count)
                    nc.tensor.matmul_mx(
                        out=banks[bank][:, at : at + count],
                        lhsT=b_words[i][:, P * a : P * (a + 1)].bitcast(FP8X4),
                        lhsT_scale=b_scales[4 * (a + 1) :, P * i : P * (i + 1)],
                        rhs=h_codes[c][:, entries].bitcast(FP8X4),
                        rhs_scale=h_scales[c][:, entries],
                        start=(a == 0 and at == 0),
                        stop=(a == PASSES - 1 and at + count == size(c)),
                    )

        def gather_add(piece, scaled, dst):
            nc.vector.tensor_tensor(dst, window(piece), scaled, ALU.add)
            return dst

        def clamp(summed, dst):
            nc.scalar.activation(dst, summed, ACT.Relu)
            return dst

        def scatter(piece, new):
            i, first, last = piece
            nc.vector.tensor_copy(window(piece), new)
            if last == D:
                nc.sync.dma_start(out[P * i : P * (i + 1), :], maps[i][:])

        parts = {A: slice(0, WIDE), B: slice(WIDE, WIDE + P)}

        def gather_two(i, scaled, order, summed):
            for c in order:
                gather_add((i, c, c), scaled[c], summed[:, parts[c]])
            return summed

        def clamp_two(i, summed, new):
            for c in (A, B):
                clamp(summed[:, parts[c]], new[:, parts[c]])
            return new

        for a in range(PASSES):
            weave_gm(a)
        for a in range(PASSES):
            nc.vector.quantize_mx(out=gm_codes[a][:].bitcast(FP8X4), scales=gm_scales[a][:], in_=gm_bf[a])
        for b in range(2):
            for a in range(PASSES):
                residual_on_vector((A, a, b), 2 * a + b)
        for a in range(PASSES):
            quantize_h(A, WIDE * a, WIDE)
        residual_on_vector((B, 0, 0), 4)
        residual_on_vector((B, 1, 0), 5)
        scaled0 = lead_back((0, A, A), 2, own("scaled", (0, A, A), "first_slot"))
        negate_wide(0, (0, 1))
        negate_wide(1, (6, 4))

        summed0 = gather_add((0, A, A), scaled0, negated[D, 0][:, :WIDE])
        picked = own("picked", (0, B, B))
        nc.vector.tensor_copy(picked, window((0, B, B)))
        h_scales[B] = sb("h_scales1", [P, PASSES * P], U8, "first_slot")
        quantize_h(B, 0, PASSES * P)
        scatter((0, A, A), clamp(summed0, own("new", (0, A, A))))

        scaled1 = {A: lead_back((1, A, A), 3, own("scaled", (1, A, A)))}
        product((0, B, B), 0)
        scaled1[B] = lead_back((1, B, B), 2, own("scaled", (1, B, B)))
        negate((D, 0, 0), 5)
        negate((D, 0, 1), 4)
        summed0 = own("summed", (0, B, B))
        nc.vector.scalar_tensor_tensor(summed0, banks[0][:, :P], steps[:, 0:1], picked, ALU.mult, ALU.add)
        summed1 = gather_two(1, scaled1, (B, A), own("summed", (1, A, B)))
        nc.scalar.activation(scaled1[B], summed0, ACT.Relu, scale=-1.0)
        nc.vector.tensor_tensor(window((0, B, B)), summed0, scaled1[B], ALU.add)
        turn_negated((C, 0, 1), 3)

        new1 = own("new", (1, A, B))
        scaled2 = {
            B: lead_back((2, B, B), 6, new1[:, parts[B]]),
            A: lead_back((2, A, A), 1, sheet_words(C, 0, 0, 1)),
        }
        clamp(summed1[:, parts[A]], new1[:, parts[A]])
        turn_negated((D, 0, 1), 1)
        summed2 = gather_two(2, scaled2, (B, A), own("summed", (2, A, B)))
        clamp(summed1[:, parts[B]], new1[:, parts[B]])
        residual_on_gpsimd((C, 0, 0), 1)
        residual_on_gpsimd((C, 1, 0), 2)
        scatter((1, A, B), new1)
        scatter((2, A, B), clamp_two(2, summed2, own("new", (2, A, B))))
        add_field((C, 0, 1), 3, rounded_c[:])
        turn_back((C, 0, 1), 1, rounded_c[:], 2)

        scaled3 = {
            B: lead_back((3, B, B), 0, own("scaled", (3, B, B), "second_slot")),
            A: lead_back((3, A, A), 7, own("scaled", (3, A, A))),
        }
        for sheet, bank in (((D, 0, 2), 3), ((D, 1, 0), 2)):
            negate(sheet, bank)
            turn_negated(sheet, bank)
        negate((D, 1, 1), 0)
        negate((D, 1, 2), 7)
        summed3 = gather_two(3, scaled3, (B, A), negated[C, 1][:, : WIDE + P])
        h_scales[C] = sb("h_scales2", [P, PASSES * WIDE], U8, "second_slot")
        quantize_h(C, 0, PASSES * WIDE)
        residual_on_gpsimd((D, 0, 0), 1)
        scatter((3, A, B), clamp_two(3, summed3, own("new", (3, A, B))))
        add_field((D, 0, 1), 1, rounded_d[:, :WIDE])
        add_field((D, 0, 2), 3, rounded_d[:, WIDE:PASS])

        pieces = [(i, C, C) for i in range(TILES)]
        scaled = [
            lead_back(pieces[0], 4, own("scaled", pieces[0])),
            lead_back(pieces[1], 5, own("scaled", pieces[1])),
            lead_back(pieces[2], 7, sheet_words(D, 1, 1, 1)),
        ]
        turn_back((D, 0, 1), 2, rounded_d[:, :PASS], 7)
        summed = [gather_add(pieces[i], scaled[i], own("summed", pieces[i])) for i in range(3)]
        residual_on_gpsimd((D, 1, 1), 2)
        scatter(pieces[0], clamp(summed[0], scaled[1]))
        scatter(pieces[1], clamp(summed[1], own("new", pieces[1])))
        add_field((D, 1, 0), 2, rounded_d[:, PASS:])
        turn_back((D, 1, 0), 1, rounded_d[:, PASS:], 7)
        h_scales[D] = sb("h_scales3", [P, PASSES * size(D)], U8, "field%d_%d" % (D, 1))
        for a in range(PASSES):
            quantize_h(D, size(D) * a, size(D))
        last = gather_add(pieces[3], lead_back(pieces[3], 7, own("scaled", pieces[3])), negated[D, 1][:, PACK * size(D) - WIDE :])
        scatter(pieces[2], clamp(summed[2], sheet_words(D, 0, 0, 1)))
        scatter(pieces[3], clamp(last, own("new", pieces[3])))

        pieces = [(i, D, D) for i in range(TILES)]
        scaled = [lead_back(pieces[i], (4, 5, 3)[i], own("scaled", pieces[i])) for i in range(3)]
        summed = [gather_add(pieces[i], scaled[i], own("summed", pieces[i])) for i in range(3)]
        scatter(pieces[0], clamp(summed[0], scaled[1]))
        summed.append(gather_add(pieces[3], lead_back(pieces[3], 1, summed[0]), own("summed", pieces[3])))
        for i in range(1, TILES):
            scatter(pieces[i], clamp(summed[i], own("new", pieces[i])))
